import numpy as np
import ml_dtypes


def mxq(x, axis, fmt="e4m3"):
    dtype, down = {"e4m3": (ml_dtypes.float8_e4m3fn, 7), "e5m2": (ml_dtypes.float8_e5m2, 14)}[fmt]
    v = np.moveaxis(np.asarray(x, np.float32).astype(ml_dtypes.bfloat16).astype(np.float64), axis, -1)
    blocks = v.reshape(v.shape[:-1] + (-1, 32))
    amax = np.abs(blocks).max(-1, keepdims=True)
    byte = np.maximum(np.where(amax > 0, np.frexp(amax)[1] - 1 + 127, 0) - down, 1)
    scale = np.exp2(byte - 127.0)
    codes = (blocks / scale).astype(np.float32).astype(dtype).astype(np.float64)
    return np.moveaxis((codes * scale).reshape(v.shape), -1, axis)


WIDE = False


def mx_kscale(k):
    if not WIDE:
        return np.ones(k)
    levels = np.array([10, -10, 5, -5, 0])
    if k % 512:
        return np.exp2(np.random.permutation(np.resize(levels, k // 32))).repeat(32)
    a = np.empty((k // 512, 16))
    for p in range(k // 512):
        a[p, :8] = np.random.permutation(np.resize(levels, 8))
        for g in range(8):
            far = levels[np.abs(levels - a[p, g]) >= 10]
            a[p, g + 8] = far[np.random.randint(len(far))]
    return np.exp2(a.ravel()).repeat(32)


def f64(x):
    return np.asarray(x).astype(np.float64)


def striped(idx):
    return np.tile(idx.reshape(-1, 16).T, (8, 1)).astype(np.uint16)


def unstriped(offs):
    return offs[:16].T.reshape(-1).astype(np.int64)


E2M1 = np.array([0.0, 0.5, 1.0, 1.5, 2.0, 3.0, 4.0, 6.0, -0.0, -0.5, -1.0, -1.5, -2.0, -3.0, -4.0, -6.0])


def pack_weight(w, fmt):
    k, n = w.shape
    w = f64(np.asarray(w, np.float32).astype(ml_dtypes.bfloat16)).reshape(k // 32, 32, n)
    amax = np.abs(w).max(1)
    if fmt == "e4m3":
        byte = np.frexp(amax)[1] - 1 + 127 - 7
    else:
        mant, ex = np.frexp(amax / 6.0)
        byte = np.where(mant > 0.5, ex, ex - 1) + 127
    byte = np.clip(np.where(amax > 0, byte, 1), 1, 254)
    scaled = (w * np.exp2(127.0 - byte)[:, None, :]).reshape(k, n).astype(np.float32)
    by_word = np.ascontiguousarray(scaled.reshape(k // 512, 128, 4, n).transpose(0, 1, 3, 2))
    if fmt == "e4m3":
        words = by_word.astype(ml_dtypes.float8_e4m3fn).view(np.uint8)
    else:
        c = by_word.astype(ml_dtypes.float4_e2m1fn).view(np.uint8) & 0xF
        words = (c[..., 0::2] | (c[..., 1::2] << 4)).reshape(k // 512, 128, 2 * n)
    return np.ascontiguousarray(words), np.ascontiguousarray(byte.astype(np.uint8).reshape(k // 512, 16, n))


def unpack_weight(words, scales, fmt):
    g, _, n = scales.shape
    words = np.ascontiguousarray(words).reshape(g, 128, n, -1)
    if fmt == "e4m3":
        vals = words.view(ml_dtypes.float8_e4m3fn).astype(np.float64)
    else:
        nib = np.empty((g, 128, n, 4), np.uint8)
        nib[..., 0::2] = words & 0xF
        nib[..., 1::2] = words >> 4
        vals = E2M1[nib]
    vals = vals * np.repeat(np.exp2(scales.astype(np.float64) - 127.0), 8, axis=1)[..., None]
    return vals.transpose(0, 1, 3, 2).reshape(g * 512, n)


def gelu(v):
    return 0.5 * v * (1.0 + np.tanh(np.sqrt(2.0 / np.pi) * (v + 0.044715 * v**3)))


def bf(x):
    return np.asarray(x, np.float32).astype(ml_dtypes.bfloat16)


def planes(Y):
    n, m = Y.shape
    b = f64(bf(Y)).reshape(n // 32, 32, m)
    amax = np.abs(b).max(1)
    byte = np.clip(np.where(amax > 0, np.frexp(amax)[1] - 1 + 127 - 7, 1), 1, 254)
    codes = (b * np.exp2(127.0 - byte)[:, None, :]).reshape(n, m).astype(np.float32).astype(ml_dtypes.float8_e4m3fn).view(np.uint8)
    words = codes.reshape(n // 512, 128, 4, m).transpose(0, 1, 3, 2)
    return np.ascontiguousarray(words), np.ascontiguousarray(byte.astype(np.uint8).reshape(n // 512, 16, m))


K, H, N, T, S, P = 1024, 1024, 512, 2048, 1024, 512

def setup_inputs():
    n = np.random.standard_normal
    s = mx_kscale(K)[:, None]
    u = mx_kscale(H)[:, None]
    tab_words, tab_scales = pack_weight(n((K, T)) * s, "e4m3")
    w1 = n((K, H)) / np.sqrt(K) / s * u.T
    a4_words, a4_scales = pack_weight(0.8 * n((H, N)) / np.sqrt(H) / u, "e2m1")
    b8_words, b8_scales = pack_weight(0.55 * n((K, N)) / np.sqrt(K) / s, "e4m3")
    tilt = np.random.uniform(0.5, 1.6, N) * np.sign(n(N))
    return {
        "tab_words": tab_words, "tab_scales": tab_scales,
        "offs": striped(np.random.permutation(T)[:S]),
        "pos1": striped(np.random.permutation(S)[:P]),
        "pos2": striped(np.random.permutation(S)[:P]),
        "w1": w1.astype(np.float32),
        "load": np.random.uniform(0.3, 1.7, (H, S)).astype(np.float32),
        "a4_words": a4_words, "a4_scales": a4_scales,
        "b8_words": b8_words, "b8_scales": b8_scales,
        "slope": np.random.uniform(0.6, 3.0, N).astype(np.float32),
        "thr": n(N).astype(np.float32),
        "tilt": tilt.astype(np.float32),
        "gain": np.exp(0.8 * n(N)).astype(np.float32),
    }

def reference(tab_words, tab_scales, offs, pos1, pos2, w1, load, a4_words, a4_scales,
              b8_words, b8_scales, slope, thr, tilt, gain):
    v = unpack_weight(tab_words, tab_scales, "e4m3")[:, unstriped(offs)]
    h = f64(load) * (mxq(f64(w1), 0, "e4m3").T @ v)
    e = unpack_weight(a4_words, a4_scales, "e2m1").T @ mxq(h, 0, "e4m3")
    d = unpack_weight(b8_words, b8_scales, "e4m3").T @ v
    a = 1.0 / (1.0 + np.exp(-(f64(slope)[:, None] * e[:, unstriped(pos1)] + f64(thr)[:, None])))
    c = d[:, unstriped(pos2)]
    y = f64(gain)[:, None] * np.minimum(f64(tilt)[:, None] * a, np.sin(c))
    words, scales = planes(y)
    return y, words, scales

@@ -1,0 +1,254 @@
+from contextlib import ExitStack
+
+import concourse.mybir as mybir
+
+K, H, N, T, S, PICK = 1024, 1024, 512, 2048, 1024, 512
+FLOPS = 2 * K * H * S + 2 * H * N * S + 2 * K * N * S
+
+F32 = mybir.dt.float32
+BF16 = mybir.dt.bfloat16
+I32 = mybir.dt.int32
+U32 = mybir.dt.uint32
+U16 = mybir.dt.uint16
+U8 = mybir.dt.uint8
+FP8X4 = mybir.dt.float8_e4m3fn_x4
+FP4X4 = mybir.dt.float4_e2m1fn_x4
+ALU = mybir.AluOpType
+ACT = mybir.ActivationFunctionType
+
+P = 128
+PACK = 4
+PASS = P * PACK
+HALF = 512
+QUART = 256
+
+
+def tile_list_amplifier_channel_scores_kernel(
+    tc, tab_words, tab_scales, offs, pos1, pos2, w1, load, a4_words, a4_scales,
+    b8_words, b8_scales, slope, thr, tilt, gain, out_0, out_1, out_2,
+):
+    nc = tc.nc
+    with ExitStack() as ctx:
+        keep = ctx.enter_context(tc.tile_pool(name="keep", bufs=1))
+        ring = ctx.enter_context(tc.tile_pool(name="ring", bufs=2))
+        acc = ctx.enter_context(tc.psum_pool(name="acc", bufs=4))
+        hps = ctx.enter_context(tc.psum_pool(name="hps", bufs=4))
+
+        def kept(shape, dtype, name):
+            return keep.tile(shape, dtype, name=name, align_bytes=64)
+
+        offs_sb = keep.tile([P, S // 16], U16, name="offs_sb")
+        pos1_sb = keep.tile([P, PICK // 16], U16, name="pos1_sb")
+        pos2_sb = keep.tile([P, PICK // 16], U16, name="pos2_sb")
+        tab_w = [kept([P, T], U32, f"tab_w{a}") for a in range(2)]
+        tab_s = kept([P, T], U8, "tab_s")
+        v_w = [kept([P, S], U32, f"v_w{a}") for a in range(2)]
+        v_s = kept([P, S], U8, "v_s")
+        w_raw = {(a, b): kept([P, PACK, HALF], F32, f"w_raw{a}{b}") for a in range(2) for b in range(2)}
+        w_q = {(a, b): kept([P, HALF], U32, f"w_q{a}{b}") for a in range(2) for b in range(2)}
+        w_s = {(a, b): kept([P, HALF], U8, f"w_s{a}{b}") for a in range(2) for b in range(2)}
+        ld = {(b, u): kept([P, PACK, HALF], F32, f"ld{b}{u}") for b in range(2) for u in range(2)}
+        h_q = {(b, u): kept([P, HALF], U32, f"h_q{b}{u}") for b in range(2) for u in range(2)}
+        h_s = {(b, u): kept([P, HALF], U8, f"h_s{b}{u}") for b in range(2) for u in range(2)}
+        b8_raw = kept([P, 2 * N], U32, "b8_raw")
+        b8_w = kept([P, 2 * N], U32, "b8_w")
+        a4_raw = kept([P, 4 * N], U8, "a4_raw")
+        a4_w = kept([P, 4 * N], U8, "a4_w")
+        b8s_raw = kept([P, N], U8, "b8s_raw")
+        b8_s = kept([P, N], U8, "b8_s")
+        a4s_raw = kept([P, 2 * N], U8, "a4s_raw")
+        a4_s = kept([P, 2 * N], U8, "a4_s")
+        d_sb = [kept([P, S], F32, f"d_sb{t}") for t in range(PACK)]
+        e_sb = [kept([P, S], F32, f"e_sb{t}") for t in range(PACK)]
+        third = [w_raw[1, 1][:, t, :] for t in range(PACK)]
+        picked = [w_raw[1, 0][:, 0, :], ld[0, 0][:, 0, :], w_raw[0, 1][:, 0, :], w_raw[1, 1][:, 3, :]]
+        square = kept([P, PACK, PICK], F32, "square")
+        sat = [kept([P, PACK, QUART], F32, f"sat{u}") for u in range(2)]
+        y = [kept([P, PACK, QUART], F32, f"y{u}") for u in range(2)]
+        y_b = [kept([P, PACK * QUART], BF16, f"y_b{u}") for u in range(2)]
+        y_q = kept([P, PICK], U32, "y_q")
+        y_s = kept([P, PICK], U8, "y_s")
+        rows = {name: kept([P, PACK], F32, name) for name in
+                ("slope_sb", "thr_sb", "tilt_sb", "gain_sb", "gain_tilt", "gain3", "gain4", "root", "halves")}
+
+        nc.gpsimd.memset(tab_s[:].bitcast(I32), 0)
+        nc.gpsimd.memset(b8s_raw[:].bitcast(I32), 0)
+        nc.gpsimd.memset(a4s_raw[:].bitcast(I32), 0)
+
+        def load_words(dst, src):
+            nc.sync.dma_start(out=dst[:].bitcast(I32), in_=src.rearrange("p n t -> p (n t)").bitcast(I32))
+
+        def load_w(a, b):
+            nc.sync.dma_start(out=w_raw[a, b][:], in_=w1[PASS * a : PASS * (a + 1), HALF * b : HALF * (b + 1)].rearrange("(p j) c -> p j c", j=PACK))
+
+        def load_ld(b, u):
+            nc.sync.dma_start(out=ld[b, u][:], in_=load[PASS * b : PASS * (b + 1), HALF * u : HALF * (u + 1)].rearrange("(p t) s -> p t s", t=PACK))
+
+        def load_row(name, vec):
+            nc.sync.dma_start(out=rows[name][:], in_=vec.rearrange("(p t) -> p t", t=PACK))
+
+        nc.sync.dma_start(offs_sb[:], offs)
+        nc.sync.dma_start(pos2_sb[:], pos2)
+        for q in range(4):
+            nc.sync.dma_start(out=tab_s[32 * q : 32 * q + 8, :].bitcast(I32), in_=tab_scales[:, 4 * q : 4 * q + 4, :].bitcast(I32))
+        load_words(tab_w[0], tab_words[0])
+        load_words(tab_w[1], tab_words[1])
+        nc.sync.dma_start(out=b8_raw[:].bitcast(I32).rearrange("p (a n) -> p a n", a=2),
+                          in_=b8_words.rearrange("a p n t -> p a (n t)").bitcast(I32))
+        for q in range(4):
+            nc.sync.dma_start(out=b8s_raw[32 * q : 32 * q + 8, :].bitcast(I32), in_=b8_scales[:, 4 * q : 4 * q + 4, :].bitcast(I32))
+        load_w(0, 0)
+        load_w(1, 0)
+        nc.sync.dma_start(out=a4_raw[:].bitcast(I32).rearrange("p (a n) -> p a n", a=2),
+                          in_=a4_words.rearrange("a p n -> p a n").bitcast(I32))
+        for q in range(4):
+            nc.sync.dma_start(out=a4s_raw[32 * q : 32 * q + 4, :].bitcast(I32).rearrange("r (a c) -> r a c", a=2),
+                              in_=a4_scales[:, 4 * q : 4 * q + 4, :].rearrange("a r c -> r a c").bitcast(I32))
+        load_ld(0, 0)
+        load_w(0, 1)
+        load_row("gain_sb", gain)
+        load_row("tilt_sb", tilt)
+        load_w(1, 1)
+        load_ld(1, 0)
+        load_ld(0, 1)
+        nc.sync.dma_start(pos1_sb[:], pos1)
+        load_row("slope_sb", slope)
+        load_row("thr_sb", thr)
+        load_ld(1, 1)
+
+        nc.gpsimd.memset(rows["halves"][:], 0.5)
+        nc.gpsimd.tensor_scalar(rows["gain4"][:], rows["gain_sb"][:], 4.0, 0.0, ALU.mult, ALU.add)
+        nc.gpsimd.tensor_scalar(rows["gain3"][:], rows["gain_sb"][:], 3.0, 0.0, ALU.mult, ALU.add)
+        nc.gpsimd.tensor_tensor(rows["root"][:], rows["gain4"][:], rows["halves"][:], ALU.pow)
+        nc.gpsimd.tensor_tensor(rows["gain_tilt"][:], rows["gain_sb"][:], rows["tilt_sb"][:], ALU.mult)
+
+        def prepare_w(a, b, copy):
+            rounded = ring.tile([P, PACK * HALF], BF16, name="w_b", align_bytes=64)
+            copy(out=rounded[:].rearrange("p (t m j) -> p m j t", t=PACK, j=PACK),
+                 in_=w_raw[a, b][:].rearrange("p j (m t) -> p m j t", t=PACK))
+            nc.vector.quantize_mx(out=w_q[a, b][:].bitcast(FP8X4), scales=w_s[a, b][:], in_=rounded[:])
+
+        def v_operands(a, cols):
+            return dict(rhs=v_w[a][:, cols].bitcast(FP8X4), rhs_scale=v_s[4 * a : P, cols])
+
+        def make_h(b, u, k):
+            rounded = ring.tile([P, PACK * QUART], BF16, name="h_b", align_bytes=64, bufs=3)
+            for i in range(2):
+                c0 = QUART * k + P * i
+                bank = hps.tile([P, PACK, P], F32, name="h_bank")
+                for t in range(PACK):
+                    for a in range(2):
+                        nc.tensor.matmul_mx(out=bank[:, t, :], lhsT=w_q[a, b][:, P * t : P * (t + 1)].bitcast(FP8X4),
+                                            lhsT_scale=w_s[a, b][:, P * t : P * (t + 1)],
+                                            start=(a == 0), stop=(a == 1),
+                                            **v_operands(a, slice(HALF * u + c0, HALF * u + c0 + P)))
+                nc.vector.tensor_tensor(
+                    out=rounded[:, PASS * i : PASS * (i + 1)].rearrange("p (c e t) -> p c t e", e=4, t=PACK),
+                    in0=bank[:].rearrange("p t (c e) -> p c t e", e=4),
+                    in1=ld[b, u][:, :, c0 : c0 + P].rearrange("p t (c e) -> p c t e", e=4),
+                    op=ALU.mult)
+            cols = slice(QUART * k, QUART * (k + 1))
+            nc.vector.quantize_mx(out=h_q[b, u][:, cols].bitcast(FP8X4), scales=h_s[b, u][:, cols], in_=rounded[:])
+
+        def e_pass(out, t, b, u, cols, start, stop):
+            c0 = N * b + P * t
+            nc.tensor.matmul_mx(out=out, lhsT=a4_w[:, 2 * c0 : 2 * (c0 + P)].bitcast(FP4X4), lhsT_scale=a4_s[:, c0 : c0 + P],
+                                rhs=h_q[b, u][:, cols].bitcast(FP8X4), rhs_scale=h_s[b, u][:, cols], start=start, stop=stop)
+
+        def make_d(t):
+            for u in range(2):
+                bank = acc.tile([P, HALF], F32, name="bank")
+                for a in range(2):
+                    nc.tensor.matmul_mx(out=bank[:], lhsT=b8_w[:, N * a + P * t : N * a + P * (t + 1)].bitcast(FP8X4),
+                                        lhsT_scale=b8_s[4 * a : P, P * t : P * (t + 1)],
+                                        start=(a == 0), stop=(a == 1), **v_operands(a, slice(HALF * u, HALF * (u + 1))))
+                nc.scalar.copy(out=d_sb[t][:, HALF * u : HALF * (u + 1)], in_=bank[:])
+
+        def sine(t):
+            nc.scalar.activation(out=third[t], in_=picked[t], func=ACT.Sin, scale=-1.0 / 3.0)
+            nc.scalar.activation(out=square[:, t, :], in_=third[t], func=ACT.Square, scale=rows["root"][:, t : t + 1])
+
+        nc.vector.tensor_copy(out=v_s[:], in_=tab_s[:].indirect(offs_sb[:]))
+        nc.vector.tensor_copy(out=v_w[0][:], in_=tab_w[0][:].indirect(offs_sb[:]))
+        nc.vector.tensor_copy(out=v_w[1][:], in_=tab_w[1][:].indirect(offs_sb[:]))
+        nc.scalar.copy(out=b8_w[:].rearrange("p (a t m e) -> p a m t e", a=2, t=PACK, e=4),
+                       in_=b8_raw[:].rearrange("p (a m e t) -> p a m t e", a=2, t=PACK, e=4))
+        nc.vector.tensor_copy(out=b8_s[:].rearrange("p (t m e) -> p m t e", t=PACK, e=16),
+                              in_=b8s_raw[:].rearrange("p (m e t) -> p m t e", t=PACK, e=16))
+        prepare_w(0, 0, nc.vector.tensor_copy)
+        prepare_w(1, 0, nc.vector.tensor_copy)
+        make_d(0)
+        make_d(1)
+        make_d(2)
+        make_d(3)
+        for k in range(2):
+            make_h(0, 0, k)
+        nc.scalar.copy(out=a4_w[:].bitcast(U16).rearrange("p (a t m e) -> p a m t e", a=2, t=PACK, e=8),
+                       in_=a4_raw[:].bitcast(U16).rearrange("p (a m e t) -> p a m t e", a=2, t=PACK, e=8))
+        prepare_w(0, 1, nc.scalar.copy)
+        prepare_w(1, 1, nc.scalar.copy)
+        nc.vector.tensor_copy(out=a4_s[:].rearrange("p (a t m e) -> p a m t e", a=2, t=PACK, e=16),
+                              in_=a4s_raw[:].rearrange("p (a m e t) -> p a m t e", a=2, t=PACK, e=16))
+        first = [acc.tile([P, HALF], F32, name="bank") for t in range(PACK)]
+        for t in range(PACK):
+            e_pass(first[t][:], t, 0, 0, slice(0, HALF), True, False)
+        for k in range(2):
+            make_h(1, 0, k)
+        for t in range(PACK):
+            e_pass(first[t][:], t, 1, 0, slice(0, HALF), False, True)
+            nc.scalar.copy(out=e_sb[t][:, 0:HALF], in_=first[t][:])
+        for k in range(2):
+            make_h(0, 1, k)
+        nc.vector.tensor_copy(out=picked[0], in_=d_sb[0][:].indirect(pos2_sb[:]))
+        nc.vector.tensor_copy(out=picked[1], in_=d_sb[1][:].indirect(pos2_sb[:]))
+        nc.vector.tensor_copy(out=picked[2], in_=d_sb[2][:].indirect(pos2_sb[:]))
+        nc.vector.tensor_copy(out=picked[3], in_=d_sb[3][:].indirect(pos2_sb[:]))
+        sine(0)
+        sine(1)
+        sine(2)
+        sine(3)
+        banks = {}
+        for k in range(2):
+            for g in range(2):
+                banks[k, g] = acc.tile([P, 2, QUART], F32, name="bank")
+                for i in range(2):
+                    e_pass(banks[k, g][:, i, :], 2 * g + i, 0, 1, slice(QUART * k, QUART * (k + 1)), i == 0, False)
+
+        def fetch_e(k, t, copy):
+            copy(out=e_sb[t][:, HALF + QUART * k : HALF + QUART * (k + 1)], in_=banks[k, t // 2][:, t % 2, :])
+
+        for k in range(2):
+            make_h(1, 1, k)
+            for g in range(2):
+                for i in range(2):
+                    e_pass(banks[k, g][:, i, :], 2 * g + i, 1, 1, slice(QUART * k, QUART * (k + 1)), False, i == 1)
+            if k == 0:
+                fetch_e(0, 0, nc.scalar.copy)
+                fetch_e(0, 1, nc.scalar.copy)
+                fetch_e(0, 2, nc.scalar.copy)
+                fetch_e(0, 3, nc.scalar.copy)
+        fetch_e(1, 0, nc.vector.tensor_copy)
+        fetch_e(1, 2, nc.vector.tensor_copy)
+
+        ripple = ld[1, 1]
+        out_rows = out_0.rearrange("(p t) m -> p t m", t=PACK)
+        out_words = out_1[0].rearrange("p m t -> p (m t)").bitcast(I32)
+        for u in range(2):
+            cols = slice(QUART * u, QUART * (u + 1))
+            for t in range(PACK):
+                if u == 0 and t in (1, 3,):
+                    fetch_e(1, t, nc.scalar.copy)
+                nc.scalar.activation(out=sat[u][:, t, :], in_=e_sb[t][:].indirect(pos1_sb[:, 16 * u : 16 * (u + 1)]), func=ACT.Sigmoid,
+                                     bias=rows["thr_sb"][:, t : t + 1], scale=rows["slope_sb"][:, t : t + 1])
+                nc.vector.scalar_tensor_tensor(out=ripple[:, t, cols], in0=square[:, t, cols], scalar=rows["gain3"][:, t : t + 1],
+                                               in1=third[t][:, cols], op0=ALU.subtract, op1=ALU.mult)
+                nc.vector.scalar_tensor_tensor(out=y[u][:, t, :], in0=sat[u][:, t, :], scalar=rows["gain_tilt"][:, t : t + 1],
+                                               in1=ripple[:, t, cols], op0=ALU.mult, op1=ALU.min)
+            nc.sync.dma_start(out=out_rows[:, :, cols], in_=y[u][:])
+            nc.vector.tensor_copy(out=y_b[u][:].rearrange("p (c e t) -> p c t e", e=4, t=PACK),
+                                  in_=y[u][:].rearrange("p t (c e) -> p c t e", e=4))
+            nc.vector.quantize_mx(out=y_q[:, cols].bitcast(FP8X4), scales=y_s[:, cols], in_=y_b[u][:])
+            nc.sync.dma_start(out=out_words[:, cols], in_=y_q[:, cols].bitcast(I32))
+        for q in range(4):
+            eng = nc.sync if q % 2 == 0 else nc.scalar
+            eng.dma_start(out=out_2[0, 4 * q : 4 * q + 4, :].bitcast(I32), in_=y_s[32 * q : 32 * q + 4, :].bitcast(I32))

@@ -54,8 +54,6 @@ def tile_list_amplifier_channel_scores_kernel(
         b8_w = kept([P, 2 * N], U32, "b8_w")
         a4_raw = kept([P, 4 * N], U8, "a4_raw")
         a4_w = kept([P, 4 * N], U8, "a4_w")
-        b8s_raw = kept([P, N], U8, "b8s_raw")
-        b8_s = kept([P, N], U8, "b8_s")
         a4s_raw = kept([P, 2 * N], U8, "a4s_raw")
         a4_s = kept([P, 2 * N], U8, "a4_s")
         d_sb = [kept([P, S], F32, f"d_sb{t}") for t in range(PACK)]
@@ -72,7 +70,6 @@ def tile_list_amplifier_channel_scores_kernel(
                 ("slope_sb", "thr_sb", "tilt_sb", "gain_sb", "gain_tilt", "gain3", "gain4", "root", "halves")}
 
         nc.gpsimd.memset(tab_s[:].bitcast(I32), 0)
-        nc.gpsimd.memset(b8s_raw[:].bitcast(I32), 0)
         nc.gpsimd.memset(a4s_raw[:].bitcast(I32), 0)
 
         def load_words(dst, src):
@@ -85,36 +82,36 @@ def tile_list_amplifier_channel_scores_kernel(
             nc.sync.dma_start(out=ld[b, u][:], in_=load[PASS * b : PASS * (b + 1), HALF * u : HALF * (u + 1)].rearrange("(p t) s -> p t s", t=PACK))
 
         def load_row(name, vec):
-            nc.sync.dma_start(out=rows[name][:], in_=vec.rearrange("(p t) -> p t", t=PACK))
+            nc.gpsimd.dma_start(out=rows[name][:], in_=vec.rearrange("(p t) -> p t", t=PACK))
 
         nc.sync.dma_start(offs_sb[:], offs)
         nc.sync.dma_start(pos2_sb[:], pos2)
         for q in range(4):
             nc.sync.dma_start(out=tab_s[32 * q : 32 * q + 8, :].bitcast(I32), in_=tab_scales[:, 4 * q : 4 * q + 4, :].bitcast(I32))
         load_words(tab_w[0], tab_words[0])
+        for q in range(4):
+            nc.sync.dma_start(out=a4s_raw[32 * q : 32 * q + 4, :].bitcast(I32).rearrange("r (a c) -> r a c", a=2),
+                              in_=a4_scales[:, 4 * q : 4 * q + 4, :].rearrange("a r c -> r a c").bitcast(I32))
         load_words(tab_w[1], tab_words[1])
+        for q in range(4):
+            nc.sync.dma_start(out=a4s_raw[32 * q + 4 : 32 * q + 12, 0:N].bitcast(I32), in_=b8_scales[:, 4 * q : 4 * q + 4, :].bitcast(I32))
         nc.sync.dma_start(out=b8_raw[:].bitcast(I32).rearrange("p (a n) -> p a n", a=2),
                           in_=b8_words.rearrange("a p n t -> p a (n t)").bitcast(I32))
-        for q in range(4):
-            nc.sync.dma_start(out=b8s_raw[32 * q : 32 * q + 8, :].bitcast(I32), in_=b8_scales[:, 4 * q : 4 * q + 4, :].bitcast(I32))
         load_w(0, 0)
         load_w(1, 0)
         nc.sync.dma_start(out=a4_raw[:].bitcast(I32).rearrange("p (a n) -> p a n", a=2),
                           in_=a4_words.rearrange("a p n -> p a n").bitcast(I32))
-        for q in range(4):
-            nc.sync.dma_start(out=a4s_raw[32 * q : 32 * q + 4, :].bitcast(I32).rearrange("r (a c) -> r a c", a=2),
-                              in_=a4_scales[:, 4 * q : 4 * q + 4, :].rearrange("a r c -> r a c").bitcast(I32))
         load_ld(0, 0)
         load_w(0, 1)
-        load_row("gain_sb", gain)
-        load_row("tilt_sb", tilt)
         load_w(1, 1)
         load_ld(1, 0)
         load_ld(0, 1)
         nc.sync.dma_start(pos1_sb[:], pos1)
+        load_ld(1, 1)
+        load_row("gain_sb", gain)
+        load_row("tilt_sb", tilt)
         load_row("slope_sb", slope)
         load_row("thr_sb", thr)
-        load_ld(1, 1)
 
         nc.gpsimd.memset(rows["halves"][:], 0.5)
         nc.gpsimd.tensor_scalar(rows["gain4"][:], rows["gain_sb"][:], 4.0, 0.0, ALU.mult, ALU.add)
@@ -136,16 +133,17 @@ def tile_list_amplifier_channel_scores_kernel(
             for i in range(2):
                 c0 = QUART * k + P * i
                 bank = hps.tile([P, PACK, P], F32, name="h_bank")
-                for t in range(PACK):
-                    for a in range(2):
+                steps = [(a, t) for a in range(2) for t in range(PACK)] if (b, u) == (1, 0) else [(a, t) for t in range(PACK) for a in range(2)]
+                for n, (a, t) in enumerate(steps):
+                    if True:
                         nc.tensor.matmul_mx(out=bank[:, t, :], lhsT=w_q[a, b][:, P * t : P * (t + 1)].bitcast(FP8X4),
                                             lhsT_scale=w_s[a, b][:, P * t : P * (t + 1)],
-                                            start=(a == 0), stop=(a == 1),
+                                            start=(n == 0), stop=(n == len(steps) - 1),
                                             **v_operands(a, slice(HALF * u + c0, HALF * u + c0 + P)))
                 nc.vector.tensor_tensor(
-                    out=rounded[:, PASS * i : PASS * (i + 1)].rearrange("p (c e t) -> p c t e", e=4, t=PACK),
-                    in0=bank[:].rearrange("p t (c e) -> p c t e", e=4),
-                    in1=ld[b, u][:, :, c0 : c0 + P].rearrange("p t (c e) -> p c t e", e=4),
+                    out=rounded[:, PASS * i : PASS * (i + 1)].rearrange("p (c e t) -> p c t e", e=2, t=PACK),
+                    in0=bank[:].rearrange("p t (c e) -> p c t e", e=2),
+                    in1=ld[b, u][:, :, c0 : c0 + P].rearrange("p t (c e) -> p c t e", e=2),
                     op=ALU.mult)
             cols = slice(QUART * k, QUART * (k + 1))
             nc.vector.quantize_mx(out=h_q[b, u][:, cols].bitcast(FP8X4), scales=h_s[b, u][:, cols], in_=rounded[:])
@@ -160,7 +158,7 @@ def tile_list_amplifier_channel_scores_kernel(
                 bank = acc.tile([P, HALF], F32, name="bank")
                 for a in range(2):
                     nc.tensor.matmul_mx(out=bank[:], lhsT=b8_w[:, N * a + P * t : N * a + P * (t + 1)].bitcast(FP8X4),
-                                        lhsT_scale=b8_s[4 * a : P, P * t : P * (t + 1)],
+                                        lhsT_scale=a4_s[4 + 4 * a : P, P * t : P * (t + 1)],
                                         start=(a == 0), stop=(a == 1), **v_operands(a, slice(HALF * u, HALF * (u + 1))))
                 nc.scalar.copy(out=d_sb[t][:, HALF * u : HALF * (u + 1)], in_=bank[:])
 
@@ -173,8 +171,8 @@ def tile_list_amplifier_channel_scores_kernel(
         nc.vector.tensor_copy(out=v_w[1][:], in_=tab_w[1][:].indirect(offs_sb[:]))
         nc.scalar.copy(out=b8_w[:].rearrange("p (a t m e) -> p a m t e", a=2, t=PACK, e=4),
                        in_=b8_raw[:].rearrange("p (a m e t) -> p a m t e", a=2, t=PACK, e=4))
-        nc.vector.tensor_copy(out=b8_s[:].rearrange("p (t m e) -> p m t e", t=PACK, e=16),
-                              in_=b8s_raw[:].rearrange("p (m e t) -> p m t e", t=PACK, e=16))
+        nc.vector.tensor_copy(out=a4_s[:].rearrange("p (a t m e) -> p a m t e", a=2, t=PACK, e=16),
+                              in_=a4s_raw[:].rearrange("p (a m e t) -> p a m t e", a=2, t=PACK, e=16))
         prepare_w(0, 0, nc.vector.tensor_copy)
         prepare_w(1, 0, nc.vector.tensor_copy)
         make_d(0)
@@ -187,8 +185,6 @@ def tile_list_amplifier_channel_scores_kernel(
                        in_=a4_raw[:].bitcast(U16).rearrange("p (a m e t) -> p a m t e", a=2, t=PACK, e=8))
         prepare_w(0, 1, nc.scalar.copy)
         prepare_w(1, 1, nc.scalar.copy)
-        nc.vector.tensor_copy(out=a4_s[:].rearrange("p (a t m e) -> p a m t e", a=2, t=PACK, e=16),
-                              in_=a4s_raw[:].rearrange("p (a m e t) -> p a m t e", a=2, t=PACK, e=16))
         first = [acc.tile([P, HALF], F32, name="bank") for t in range(PACK)]
         for t in range(PACK):
             e_pass(first[t][:], t, 0, 0, slice(0, HALF), True, False)
@@ -228,25 +224,30 @@ def tile_list_amplifier_channel_scores_kernel(
                 fetch_e(0, 2, nc.scalar.copy)
                 fetch_e(0, 3, nc.scalar.copy)
         fetch_e(1, 0, nc.vector.tensor_copy)
+        fetch_e(1, 1, nc.vector.tensor_copy)
         fetch_e(1, 2, nc.vector.tensor_copy)
+        fetch_e(1, 3, nc.vector.tensor_copy)
 
         ripple = ld[1, 1]
+        for u in range(2):
+            cols = slice(QUART * u, QUART * (u + 1))
+            for t in range(PACK):
+                nc.vector.scalar_tensor_tensor(out=ripple[:, t, cols], in0=square[:, t, cols], scalar=rows["gain3"][:, t : t + 1],
+                                               in1=third[t][:, cols], op0=ALU.subtract, op1=ALU.mult)
         out_rows = out_0.rearrange("(p t) m -> p t m", t=PACK)
         out_words = out_1[0].rearrange("p m t -> p (m t)").bitcast(I32)
         for u in range(2):
             cols = slice(QUART * u, QUART * (u + 1))
             for t in range(PACK):
-                if u == 0 and t in (1, 3,):
+                if u == 0 and t in ():
                     fetch_e(1, t, nc.scalar.copy)
                 nc.scalar.activation(out=sat[u][:, t, :], in_=e_sb[t][:].indirect(pos1_sb[:, 16 * u : 16 * (u + 1)]), func=ACT.Sigmoid,
                                      bias=rows["thr_sb"][:, t : t + 1], scale=rows["slope_sb"][:, t : t + 1])
-                nc.vector.scalar_tensor_tensor(out=ripple[:, t, cols], in0=square[:, t, cols], scalar=rows["gain3"][:, t : t + 1],
-                                               in1=third[t][:, cols], op0=ALU.subtract, op1=ALU.mult)
                 nc.vector.scalar_tensor_tensor(out=y[u][:, t, :], in0=sat[u][:, t, :], scalar=rows["gain_tilt"][:, t : t + 1],
                                                in1=ripple[:, t, cols], op0=ALU.mult, op1=ALU.min)
             nc.sync.dma_start(out=out_rows[:, :, cols], in_=y[u][:])
-            nc.vector.tensor_copy(out=y_b[u][:].rearrange("p (c e t) -> p c t e", e=4, t=PACK),
-                                  in_=y[u][:].rearrange("p t (c e) -> p c t e", e=4))
+            nc.vector.tensor_copy(out=y_b[u][:].rearrange("p (c e t) -> p c t e", e=2, t=PACK),
+                                  in_=y[u][:].rearrange("p t (c e) -> p c t e", e=2))
             nc.vector.quantize_mx(out=y_q[:, cols].bitcast(FP8X4), scales=y_s[:, cols], in_=y_b[u][:])
             nc.sync.dma_start(out=out_words[:, cols], in_=y_q[:, cols].bitcast(I32))
         for q in range(4):

@@ -45,6 +45,7 @@ def tile_list_amplifier_channel_scores_kernel(
         v_w = [kept([P, S], U32, f"v_w{a}") for a in range(2)]
         v_s = kept([P, S], U8, "v_s")
         w_raw = {(a, b): kept([P, PACK, HALF], F32, f"w_raw{a}{b}") for a in range(2) for b in range(2)}
+        w_b = {(a, b): kept([P, PACK * HALF], BF16, f"w_b{a}{b}") for a in range(2) for b in range(2)}
         w_q = {(a, b): kept([P, HALF], U32, f"w_q{a}{b}") for a in range(2) for b in range(2)}
         w_s = {(a, b): kept([P, HALF], U8, f"w_s{a}{b}") for a in range(2) for b in range(2)}
         ld = {(b, u): kept([P, PACK, HALF], F32, f"ld{b}{u}") for b in range(2) for u in range(2)}
@@ -59,7 +60,7 @@ def tile_list_amplifier_channel_scores_kernel(
         d_sb = [kept([P, S], F32, f"d_sb{t}") for t in range(PACK)]
         e_sb = [kept([P, S], F32, f"e_sb{t}") for t in range(PACK)]
         third = [w_raw[1, 1][:, t, :] for t in range(PACK)]
-        picked = [w_raw[1, 0][:, 0, :], ld[0, 0][:, 0, :], w_raw[0, 1][:, 0, :], w_raw[1, 1][:, 3, :]]
+        picked = [w_b[0, 0][:].bitcast(F32)[:, 0:PICK], w_b[1, 0][:].bitcast(F32)[:, 0:PICK], ld[0, 0][:, 0, :], ld[0, 0][:, 1, :]]
         square = kept([P, PACK, PICK], F32, "square")
         sat = [kept([P, PACK, QUART], F32, f"sat{u}") for u in range(2)]
         y = [kept([P, PACK, QUART], F32, f"y{u}") for u in range(2)]
@@ -99,13 +100,13 @@ def tile_list_amplifier_channel_scores_kernel(
                           in_=b8_words.rearrange("a p n t -> p a (n t)").bitcast(I32))
         load_w(0, 0)
         load_w(1, 0)
-        nc.sync.dma_start(out=a4_raw[:].bitcast(I32).rearrange("p (a n) -> p a n", a=2),
-                          in_=a4_words.rearrange("a p n -> p a n").bitcast(I32))
         load_ld(0, 0)
         load_w(0, 1)
         load_w(1, 1)
-        load_ld(1, 0)
+        nc.sync.dma_start(out=a4_raw[:].bitcast(I32).rearrange("p (a n) -> p a n", a=2),
+                          in_=a4_words.rearrange("a p n -> p a n").bitcast(I32))
         load_ld(0, 1)
+        load_ld(1, 0)
         nc.sync.dma_start(pos1_sb[:], pos1)
         load_ld(1, 1)
         load_row("gain_sb", gain)
@@ -119,10 +120,11 @@ def tile_list_amplifier_channel_scores_kernel(
         nc.gpsimd.tensor_tensor(rows["root"][:], rows["gain4"][:], rows["halves"][:], ALU.pow)
         nc.gpsimd.tensor_tensor(rows["gain_tilt"][:], rows["gain_sb"][:], rows["tilt_sb"][:], ALU.mult)
 
-        def prepare_w(a, b, copy):
-            rounded = ring.tile([P, PACK * HALF], BF16, name="w_b", align_bytes=64)
-            copy(out=rounded[:].rearrange("p (t m j) -> p m j t", t=PACK, j=PACK),
-                 in_=w_raw[a, b][:].rearrange("p j (m t) -> p m j t", t=PACK))
+        def prepare_w(a, b, copies):
+            rounded = w_b[a, b]
+            for g, copy in enumerate(copies):
+                copy(out=rounded[:].rearrange("p (t m j) -> p m j t", t=PACK, j=PACK)[:, :, :, 2 * g : 2 * g + 2],
+                     in_=w_raw[a, b][:].rearrange("p j (m t) -> p m j t", t=PACK)[:, :, :, 2 * g : 2 * g + 2])
             nc.vector.quantize_mx(out=w_q[a, b][:].bitcast(FP8X4), scales=w_s[a, b][:], in_=rounded[:])
 
         def v_operands(a, cols):
@@ -132,7 +134,7 @@ def tile_list_amplifier_channel_scores_kernel(
             rounded = ring.tile([P, PACK * QUART], BF16, name="h_b", align_bytes=64, bufs=3)
             for i in range(2):
                 c0 = QUART * k + P * i
-                bank = hps.tile([P, PACK, P], F32, name="h_bank")
+                bank = acc.tile([P, PACK, P], F32, name="bank") if (b, u) == (0, 1) else hps.tile([P, PACK, P], F32, name="h_bank")
                 steps = [(a, t) for a in range(2) for t in range(PACK)] if (b, u) == (1, 0) else [(a, t) for t in range(PACK) for a in range(2)]
                 for n, (a, t) in enumerate(steps):
                     if True:
@@ -166,6 +168,23 @@ def tile_list_amplifier_channel_scores_kernel(
             nc.scalar.activation(out=third[t], in_=picked[t], func=ACT.Sin, scale=-1.0 / 3.0)
             nc.scalar.activation(out=square[:, t, :], in_=third[t], func=ACT.Square, scale=rows["root"][:, t : t + 1])
 
+        banks = {}
+
+        def open_e(n):
+            u, k = divmod(n, 2)
+            for g in range(2):
+                banks[n, g] = acc.tile([P, 2, QUART], F32, name="bank")
+                for i in range(2):
+                    e_pass(banks[n, g][:, i, :], 2 * g + i, 0, u, slice(QUART * k, QUART * (k + 1)), i == 0, False)
+
+        def close_e(n, copy):
+            u, k = divmod(n, 2)
+            for g in range(2):
+                for i in range(2):
+                    e_pass(banks[n, g][:, i, :], 2 * g + i, 1, u, slice(QUART * k, QUART * (k + 1)), False, i == 1)
+            for t in range(PACK):
+                copy(out=e_sb[t][:, QUART * n : QUART * (n + 1)], in_=banks[n, t // 2][:, t % 2, :])
+
         nc.vector.tensor_copy(out=v_s[:], in_=tab_s[:].indirect(offs_sb[:]))
         nc.vector.tensor_copy(out=v_w[0][:], in_=tab_w[0][:].indirect(offs_sb[:]))
         nc.vector.tensor_copy(out=v_w[1][:], in_=tab_w[1][:].indirect(offs_sb[:]))
@@ -173,28 +192,32 @@ def tile_list_amplifier_channel_scores_kernel(
                        in_=b8_raw[:].rearrange("p (a m e t) -> p a m t e", a=2, t=PACK, e=4))
         nc.vector.tensor_copy(out=a4_s[:].rearrange("p (a t m e) -> p a m t e", a=2, t=PACK, e=16),
                               in_=a4s_raw[:].rearrange("p (a m e t) -> p a m t e", a=2, t=PACK, e=16))
-        prepare_w(0, 0, nc.vector.tensor_copy)
-        prepare_w(1, 0, nc.vector.tensor_copy)
+        prepare_w(0, 0, (nc.vector.tensor_copy, nc.vector.tensor_copy))
+        prepare_w(1, 0, (nc.scalar.copy, nc.vector.tensor_copy))
         make_d(0)
         make_d(1)
         make_d(2)
         make_d(3)
-        for k in range(2):
-            make_h(0, 0, k)
+        make_h(0, 0, 0)
+        make_h(0, 0, 1)
+        prepare_w(0, 1, (nc.scalar.copy, nc.scalar.copy))
+        prepare_w(1, 1, (nc.scalar.copy, nc.scalar.copy))
         nc.scalar.copy(out=a4_w[:].bitcast(U16).rearrange("p (a t m e) -> p a m t e", a=2, t=PACK, e=8),
                        in_=a4_raw[:].bitcast(U16).rearrange("p (a m e t) -> p a m t e", a=2, t=PACK, e=8))
-        prepare_w(0, 1, nc.scalar.copy)
-        prepare_w(1, 1, nc.scalar.copy)
-        first = [acc.tile([P, HALF], F32, name="bank") for t in range(PACK)]
-        for t in range(PACK):
-            e_pass(first[t][:], t, 0, 0, slice(0, HALF), True, False)
-        for k in range(2):
-            make_h(1, 0, k)
-        for t in range(PACK):
-            e_pass(first[t][:], t, 1, 0, slice(0, HALF), False, True)
-            nc.scalar.copy(out=e_sb[t][:, 0:HALF], in_=first[t][:])
-        for k in range(2):
-            make_h(0, 1, k)
+        make_h(0, 1, 0)
+        make_h(0, 1, 1)
+        make_h(1, 0, 0)
+        open_e(0)
+        open_e(1)
+        close_e(0, nc.scalar.copy)
+        make_h(1, 0, 1)
+        close_e(1, nc.scalar.copy)
+        make_h(1, 1, 0)
+        open_e(2)
+        close_e(2, nc.scalar.copy)
+        make_h(1, 1, 1)
+        open_e(3)
+        close_e(3, nc.vector.tensor_copy)
         nc.vector.tensor_copy(out=picked[0], in_=d_sb[0][:].indirect(pos2_sb[:]))
         nc.vector.tensor_copy(out=picked[1], in_=d_sb[1][:].indirect(pos2_sb[:]))
         nc.vector.tensor_copy(out=picked[2], in_=d_sb[2][:].indirect(pos2_sb[:]))
@@ -203,30 +226,6 @@ def tile_list_amplifier_channel_scores_kernel(
         sine(1)
         sine(2)
         sine(3)
-        banks = {}
-        for k in range(2):
-            for g in range(2):
-                banks[k, g] = acc.tile([P, 2, QUART], F32, name="bank")
-                for i in range(2):
-                    e_pass(banks[k, g][:, i, :], 2 * g + i, 0, 1, slice(QUART * k, QUART * (k + 1)), i == 0, False)
-
-        def fetch_e(k, t, copy):
-            copy(out=e_sb[t][:, HALF + QUART * k : HALF + QUART * (k + 1)], in_=banks[k, t // 2][:, t % 2, :])
-
-        for k in range(2):
-            make_h(1, 1, k)
-            for g in range(2):
-                for i in range(2):
-                    e_pass(banks[k, g][:, i, :], 2 * g + i, 1, 1, slice(QUART * k, QUART * (k + 1)), False, i == 1)
-            if k == 0:
-                fetch_e(0, 0, nc.scalar.copy)
-                fetch_e(0, 1, nc.scalar.copy)
-                fetch_e(0, 2, nc.scalar.copy)
-                fetch_e(0, 3, nc.scalar.copy)
-        fetch_e(1, 0, nc.vector.tensor_copy)
-        fetch_e(1, 1, nc.vector.tensor_copy)
-        fetch_e(1, 2, nc.vector.tensor_copy)
-        fetch_e(1, 3, nc.vector.tensor_copy)
 
         ripple = ld[1, 1]
         for u in range(2):
@@ -239,17 +238,16 @@ def tile_list_amplifier_channel_scores_kernel(
         for u in range(2):
             cols = slice(QUART * u, QUART * (u + 1))
             for t in range(PACK):
-                if u == 0 and t in ():
-                    fetch_e(1, t, nc.scalar.copy)
                 nc.scalar.activation(out=sat[u][:, t, :], in_=e_sb[t][:].indirect(pos1_sb[:, 16 * u : 16 * (u + 1)]), func=ACT.Sigmoid,
                                      bias=rows["thr_sb"][:, t : t + 1], scale=rows["slope_sb"][:, t : t + 1])
                 nc.vector.scalar_tensor_tensor(out=y[u][:, t, :], in0=sat[u][:, t, :], scalar=rows["gain_tilt"][:, t : t + 1],
                                                in1=ripple[:, t, cols], op0=ALU.mult, op1=ALU.min)
-            nc.sync.dma_start(out=out_rows[:, :, cols], in_=y[u][:])
+                if t % 2 == 1:
+                    nc.sync.dma_start(out=out_rows[:, t - 1 : t + 1, cols], in_=y[u][:, t - 1 : t + 1, :])
             nc.vector.tensor_copy(out=y_b[u][:].rearrange("p (c e t) -> p c t e", e=2, t=PACK),
                                   in_=y[u][:].rearrange("p t (c e) -> p c t e", e=2))
             nc.vector.quantize_mx(out=y_q[:, cols].bitcast(FP8X4), scales=y_s[:, cols], in_=y_b[u][:])
-            nc.sync.dma_start(out=out_words[:, cols], in_=y_q[:, cols].bitcast(I32))
+            (nc.sync, nc.scalar)[u].dma_start(out=out_words[:, cols], in_=y_q[:, cols].bitcast(I32))
         for q in range(4):
-            eng = nc.sync if q % 2 == 0 else nc.scalar
+            eng = nc.sync if q < 3 else nc.scalar
             eng.dma_start(out=out_2[0, 4 * q : 4 * q + 4, :].bitcast(I32), in_=y_s[32 * q : 32 * q + 4, :].bitcast(I32))

@@ -45,9 +45,12 @@ def tile_list_amplifier_channel_scores_kernel(
         v_w = [kept([P, S], U32, f"v_w{a}") for a in range(2)]
         v_s = kept([P, S], U8, "v_s")
         w_raw = {(a, b): kept([P, PACK, HALF], F32, f"w_raw{a}{b}") for a in range(2) for b in range(2)}
-        w_b = {(a, b): kept([P, PACK * HALF], BF16, f"w_b{a}{b}") for a in range(2) for b in range(2)}
-        w_q = {(a, b): kept([P, HALF], U32, f"w_q{a}{b}") for a in range(2) for b in range(2)}
-        w_s = {(a, b): kept([P, HALF], U8, f"w_s{a}{b}") for a in range(2) for b in range(2)}
+        w_bb = [kept([P, 2, PACK * HALF], BF16, f"w_b{b}") for b in range(2)]
+        w_b = {(a, b): w_bb[b][:, a, :] for a in range(2) for b in range(2)}
+        w_qq = [kept([P, 2 * HALF], U32, f"w_q{b}") for b in range(2)]
+        w_q = {(a, b): w_qq[b][:, HALF * a : HALF * (a + 1)] for a in range(2) for b in range(2)}
+        w_ss = [kept([P, 2 * HALF], U8, f"w_s{b}") for b in range(2)]
+        w_s = {(a, b): w_ss[b][:, HALF * a : HALF * (a + 1)] for a in range(2) for b in range(2)}
         ld = {(b, u): kept([P, PACK, HALF], F32, f"ld{b}{u}") for b in range(2) for u in range(2)}
         h_q = {(b, u): kept([P, HALF], U32, f"h_q{b}{u}") for b in range(2) for u in range(2)}
         h_s = {(b, u): kept([P, HALF], U8, f"h_s{b}{u}") for b in range(2) for u in range(2)}
@@ -60,10 +63,11 @@ def tile_list_amplifier_channel_scores_kernel(
         d_sb = [kept([P, S], F32, f"d_sb{t}") for t in range(PACK)]
         e_sb = [kept([P, S], F32, f"e_sb{t}") for t in range(PACK)]
         third = [w_raw[1, 1][:, t, :] for t in range(PACK)]
-        picked = [w_b[0, 0][:].bitcast(F32)[:, 0:PICK], w_b[1, 0][:].bitcast(F32)[:, 0:PICK], ld[0, 0][:, 0, :], ld[0, 0][:, 1, :]]
+        picked = [w_b[0, 0].bitcast(F32)[:, 0:PICK], w_b[1, 0].bitcast(F32)[:, 0:PICK], ld[0, 0][:, 0, :], ld[0, 0][:, 1, :]]
+        pairs = [w_bb[0][:].bitcast(F32)[:, :, 0:PICK], ld[0, 0][:, 0:2, :]]
         square = kept([P, PACK, PICK], F32, "square")
-        sat = [kept([P, PACK, QUART], F32, f"sat{u}") for u in range(2)]
-        y = [kept([P, PACK, QUART], F32, f"y{u}") for u in range(2)]
+        sat = kept([P, PACK, PICK], F32, "sat")
+        y = kept([P, 2, PACK, QUART], F32, "y")
         y_b = [kept([P, PACK * QUART], BF16, f"y_b{u}") for u in range(2)]
         y_q = kept([P, PICK], U32, "y_q")
         y_s = kept([P, PICK], U8, "y_s")
@@ -72,6 +76,7 @@ def tile_list_amplifier_channel_scores_kernel(
 
         nc.gpsimd.memset(tab_s[:].bitcast(I32), 0)
         nc.gpsimd.memset(a4s_raw[:].bitcast(I32), 0)
+        nc.gpsimd.memset(rows["halves"][:], 0.5)
 
         def load_words(dst, src):
             nc.sync.dma_start(out=dst[:].bitcast(I32), in_=src.rearrange("p n t -> p (n t)").bitcast(I32))
@@ -114,7 +119,6 @@ def tile_list_amplifier_channel_scores_kernel(
         load_row("slope_sb", slope)
         load_row("thr_sb", thr)
 
-        nc.gpsimd.memset(rows["halves"][:], 0.5)
         nc.gpsimd.tensor_scalar(rows["gain4"][:], rows["gain_sb"][:], 4.0, 0.0, ALU.mult, ALU.add)
         nc.gpsimd.tensor_scalar(rows["gain3"][:], rows["gain_sb"][:], 3.0, 0.0, ALU.mult, ALU.add)
         nc.gpsimd.tensor_tensor(rows["root"][:], rows["gain4"][:], rows["halves"][:], ALU.pow)
@@ -122,16 +126,25 @@ def tile_list_amplifier_channel_scores_kernel(
 
         def prepare_w(a, b, copies):
             rounded = w_b[a, b]
-            for g, copy in enumerate(copies):
-                copy(out=rounded[:].rearrange("p (t m j) -> p m j t", t=PACK, j=PACK)[:, :, :, 2 * g : 2 * g + 2],
+            if copies[0] is None:
+                copies[1](out=rounded.rearrange("p (t m j) -> p m j t", t=PACK, j=PACK), in_=w_raw[a, b][:].rearrange("p j (m t) -> p m j t", t=PACK))
+            for g, copy in enumerate(copies if copies[0] else ()):
+                copy(out=rounded.rearrange("p (t m j) -> p m j t", t=PACK, j=PACK)[:, :, :, 2 * g : 2 * g + 2],
                      in_=w_raw[a, b][:].rearrange("p j (m t) -> p m j t", t=PACK)[:, :, :, 2 * g : 2 * g + 2])
-            nc.vector.quantize_mx(out=w_q[a, b][:].bitcast(FP8X4), scales=w_s[a, b][:], in_=rounded[:])
+            if b not in (1,):
+                nc.vector.quantize_mx(out=w_q[a, b].bitcast(FP8X4), scales=w_s[a, b], in_=rounded)
+            elif a == 1:
+                nc.vector.quantize_mx(out=w_qq[b][:].bitcast(FP8X4), scales=w_ss[b][:], in_=w_bb[b][:].rearrange("p a c -> p (a c)"))
 
         def v_operands(a, cols):
             return dict(rhs=v_w[a][:, cols].bitcast(FP8X4), rhs_scale=v_s[4 * a : P, cols])
 
+        wide = {}
+
         def make_h(b, u, k):
-            rounded = ring.tile([P, PACK * QUART], BF16, name="h_b", align_bytes=64, bufs=3)
+            if k == 0:
+                wide[b, u] = ring.tile([P, PACK * HALF], BF16, name="h_b", align_bytes=64)
+            rounded = wide[b, u][:, PACK * QUART * k : PACK * QUART * (k + 1)]
             for i in range(2):
                 c0 = QUART * k + P * i
                 bank = acc.tile([P, PACK, P], F32, name="bank") if (b, u) == (0, 1) else hps.tile([P, PACK, P], F32, name="h_bank")
@@ -148,7 +161,10 @@ def tile_list_amplifier_channel_scores_kernel(
                     in1=ld[b, u][:, :, c0 : c0 + P].rearrange("p t (c e) -> p c t e", e=2),
                     op=ALU.mult)
             cols = slice(QUART * k, QUART * (k + 1))
-            nc.vector.quantize_mx(out=h_q[b, u][:, cols].bitcast(FP8X4), scales=h_s[b, u][:, cols], in_=rounded[:])
+            if b == 1:
+                nc.vector.quantize_mx(out=h_q[b, u][:, cols].bitcast(FP8X4), scales=h_s[b, u][:, cols], in_=rounded)
+            elif k == 1:
+                nc.vector.quantize_mx(out=h_q[b, u][:].bitcast(FP8X4), scales=h_s[b, u][:], in_=wide[b, u][:])
 
         def e_pass(out, t, b, u, cols, start, stop):
             c0 = N * b + P * t
@@ -165,7 +181,8 @@ def tile_list_amplifier_channel_scores_kernel(
                 nc.scalar.copy(out=d_sb[t][:, HALF * u : HALF * (u + 1)], in_=bank[:])
 
         def sine(t):
-            nc.scalar.activation(out=third[t], in_=picked[t], func=ACT.Sin, scale=-1.0 / 3.0)
+            if t % 2 == 0:
+                nc.scalar.activation(out=w_raw[1, 1][:, t : t + 2, :], in_=pairs[t // 2], func=ACT.Sin, scale=-1.0 / 3.0)
             nc.scalar.activation(out=square[:, t, :], in_=third[t], func=ACT.Square, scale=rows["root"][:, t : t + 1])
 
         banks = {}
@@ -183,7 +200,7 @@ def tile_list_amplifier_channel_scores_kernel(
                 for i in range(2):
                     e_pass(banks[n, g][:, i, :], 2 * g + i, 1, u, slice(QUART * k, QUART * (k + 1)), False, i == 1)
             for t in range(PACK):
-                copy(out=e_sb[t][:, QUART * n : QUART * (n + 1)], in_=banks[n, t // 2][:, t % 2, :])
+                (copy if n < 3 else (nc.scalar.copy, nc.vector.tensor_copy, nc.vector.tensor_copy, nc.vector.tensor_copy)[t])(out=e_sb[t][:, QUART * n : QUART * (n + 1)], in_=banks[n, t // 2][:, t % 2, :])
 
         nc.vector.tensor_copy(out=v_s[:], in_=tab_s[:].indirect(offs_sb[:]))
         nc.vector.tensor_copy(out=v_w[0][:], in_=tab_w[0][:].indirect(offs_sb[:]))
@@ -192,7 +209,7 @@ def tile_list_amplifier_channel_scores_kernel(
                        in_=b8_raw[:].rearrange("p (a m e t) -> p a m t e", a=2, t=PACK, e=4))
         nc.vector.tensor_copy(out=a4_s[:].rearrange("p (a t m e) -> p a m t e", a=2, t=PACK, e=16),
                               in_=a4s_raw[:].rearrange("p (a m e t) -> p a m t e", a=2, t=PACK, e=16))
-        prepare_w(0, 0, (nc.vector.tensor_copy, nc.vector.tensor_copy))
+        prepare_w(0, 0, (None, nc.vector.tensor_copy))
         prepare_w(1, 0, (nc.scalar.copy, nc.vector.tensor_copy))
         make_d(0)
         make_d(1)
@@ -200,15 +217,23 @@ def tile_list_amplifier_channel_scores_kernel(
         make_d(3)
         make_h(0, 0, 0)
         make_h(0, 0, 1)
-        prepare_w(0, 1, (nc.scalar.copy, nc.scalar.copy))
-        prepare_w(1, 1, (nc.scalar.copy, nc.scalar.copy))
+        prepare_w(0, 1, (None, nc.scalar.copy))
+        prepare_w(1, 1, (None, nc.scalar.copy))
         nc.scalar.copy(out=a4_w[:].bitcast(U16).rearrange("p (a t m e) -> p a m t e", a=2, t=PACK, e=8),
                        in_=a4_raw[:].bitcast(U16).rearrange("p (a m e t) -> p a m t e", a=2, t=PACK, e=8))
         make_h(0, 1, 0)
         make_h(0, 1, 1)
+        nc.vector.tensor_copy(out=picked[0], in_=d_sb[0][:].indirect(pos2_sb[:]))
+        nc.vector.tensor_copy(out=picked[1], in_=d_sb[1][:].indirect(pos2_sb[:]))
+        nc.vector.tensor_copy(out=picked[2], in_=d_sb[2][:].indirect(pos2_sb[:]))
+        nc.vector.tensor_copy(out=picked[3], in_=d_sb[3][:].indirect(pos2_sb[:]))
         make_h(1, 0, 0)
         open_e(0)
         open_e(1)
+        sine(0)
+        sine(1)
+        sine(2)
+        sine(3)
         close_e(0, nc.scalar.copy)
         make_h(1, 0, 1)
         close_e(1, nc.scalar.copy)
@@ -218,36 +243,44 @@ def tile_list_amplifier_channel_scores_kernel(
         make_h(1, 1, 1)
         open_e(3)
         close_e(3, nc.vector.tensor_copy)
-        nc.vector.tensor_copy(out=picked[0], in_=d_sb[0][:].indirect(pos2_sb[:]))
-        nc.vector.tensor_copy(out=picked[1], in_=d_sb[1][:].indirect(pos2_sb[:]))
-        nc.vector.tensor_copy(out=picked[2], in_=d_sb[2][:].indirect(pos2_sb[:]))
-        nc.vector.tensor_copy(out=picked[3], in_=d_sb[3][:].indirect(pos2_sb[:]))
-        sine(0)
-        sine(1)
-        sine(2)
-        sine(3)
 
         ripple = ld[1, 1]
-        for u in range(2):
-            cols = slice(QUART * u, QUART * (u + 1))
-            for t in range(PACK):
-                nc.vector.scalar_tensor_tensor(out=ripple[:, t, cols], in0=square[:, t, cols], scalar=rows["gain3"][:, t : t + 1],
-                                               in1=third[t][:, cols], op0=ALU.subtract, op1=ALU.mult)
+        for t in range(PACK):
+            nc.vector.scalar_tensor_tensor(out=ripple[:, t, :], in0=square[:, t, :], scalar=rows["gain3"][:, t : t + 1],
+                                           in1=third[t], op0=ALU.subtract, op1=ALU.mult)
         out_rows = out_0.rearrange("(p t) m -> p t m", t=PACK)
         out_words = out_1[0].rearrange("p m t -> p (m t)").bitcast(I32)
-        for u in range(2):
+
+        def look(t, u0, u1):
+            c0, c1 = QUART * u0, QUART * u1
+            nc.scalar.activation(out=sat[:, t, c0:c1], in_=e_sb[t][:].indirect(pos1_sb[:, c0 // 16 : c1 // 16]), func=ACT.Sigmoid,
+                                 bias=rows["thr_sb"][:, t : t + 1], scale=rows["slope_sb"][:, t : t + 1])
+            nc.vector.scalar_tensor_tensor(out=y[:, u0:u1, t, :], in0=sat[:, t, c0:c1].rearrange("p (u c) -> p u c", c=QUART), scalar=rows["gain_tilt"][:, t : t + 1],
+                                           in1=ripple[:, t, c0:c1].rearrange("p (u c) -> p u c", c=QUART), op0=ALU.mult, op1=ALU.min)
+
+        def store(u, t0, t1):
+            nc.sync.dma_start(out=out_rows[:, t0:t1, QUART * u : QUART * (u + 1)], in_=y[:, u, t0:t1, :])
+
+        def planes(u):
             cols = slice(QUART * u, QUART * (u + 1))
-            for t in range(PACK):
-                nc.scalar.activation(out=sat[u][:, t, :], in_=e_sb[t][:].indirect(pos1_sb[:, 16 * u : 16 * (u + 1)]), func=ACT.Sigmoid,
-                                     bias=rows["thr_sb"][:, t : t + 1], scale=rows["slope_sb"][:, t : t + 1])
-                nc.vector.scalar_tensor_tensor(out=y[u][:, t, :], in0=sat[u][:, t, :], scalar=rows["gain_tilt"][:, t : t + 1],
-                                               in1=ripple[:, t, cols], op0=ALU.mult, op1=ALU.min)
-                if t % 2 == 1:
-                    nc.sync.dma_start(out=out_rows[:, t - 1 : t + 1, cols], in_=y[u][:, t - 1 : t + 1, :])
-            nc.vector.tensor_copy(out=y_b[u][:].rearrange("p (c e t) -> p c t e", e=2, t=PACK),
-                                  in_=y[u][:].rearrange("p t (c e) -> p c t e", e=2))
+            (nc.scalar.copy, nc.vector.tensor_copy)[u](out=y_b[u][:].rearrange("p (c e t) -> p c t e", e=2, t=PACK),
+                                  in_=y[:, u, :, :].rearrange("p t (c e) -> p c t e", e=2))
             nc.vector.quantize_mx(out=y_q[:, cols].bitcast(FP8X4), scales=y_s[:, cols], in_=y_b[u][:])
             (nc.sync, nc.scalar)[u].dma_start(out=out_words[:, cols], in_=y_q[:, cols].bitcast(I32))
+
+        WIDE = 2
+        for t in range(WIDE):
+            look(t, 0, 2)
+        for u in range(2):
+            for t in range(WIDE, PACK):
+                look(t, u, u + 1)
+                if t == 1:
+                    store(u, 0, 2)
+            if WIDE >= 2 and u == 0:
+                store(1, 0, WIDE)
+            store(u, (0 if u == 0 else WIDE) if WIDE >= 2 else 2, PACK)
+        planes(0)
+        planes(1)
         for q in range(4):
             eng = nc.sync if q < 3 else nc.scalar
             eng.dma_start(out=out_2[0, 4 * q : 4 * q + 4, :].bitcast(I32), in_=y_s[32 * q : 32 * q + 4, :].bitcast(I32))

@@ -21,6 +21,9 @@ PACK = 4
 PASS = P * PACK
 HALF = 512
 QUART = 256
+TWO = range(2)
+QUADRANTS = range(4)
+SLICES = range(PACK)
 
 
 def tile_list_amplifier_channel_scores_kernel(
@@ -30,9 +33,10 @@ def tile_list_amplifier_channel_scores_kernel(
     nc = tc.nc
     with ExitStack() as ctx:
         keep = ctx.enter_context(tc.tile_pool(name="keep", bufs=1))
+        twice = ctx.enter_context(tc.tile_pool(name="twice", bufs=1))
         ring = ctx.enter_context(tc.tile_pool(name="ring", bufs=2))
-        acc = ctx.enter_context(tc.psum_pool(name="acc", bufs=4))
-        hps = ctx.enter_context(tc.psum_pool(name="hps", bufs=4))
+        mixed_banks = ctx.enter_context(tc.psum_pool(name="mixed_banks", bufs=4))
+        h_banks = ctx.enter_context(tc.psum_pool(name="h_banks", bufs=4))
 
         def kept(shape, dtype, name):
             return keep.tile(shape, dtype, name=name, align_bytes=64)
@@ -40,247 +44,237 @@ def tile_list_amplifier_channel_scores_kernel(
         offs_sb = keep.tile([P, S // 16], U16, name="offs_sb")
         pos1_sb = keep.tile([P, PICK // 16], U16, name="pos1_sb")
         pos2_sb = keep.tile([P, PICK // 16], U16, name="pos2_sb")
-        tab_w = [kept([P, T], U32, f"tab_w{a}") for a in range(2)]
+        tab_w = [kept([P, T], U32, f"tab_w{a}") for a in TWO]
         tab_s = kept([P, T], U8, "tab_s")
-        v_w = [kept([P, S], U32, f"v_w{a}") for a in range(2)]
+        v_w = [kept([P, S], U32, f"v_w{a}") for a in TWO]
         v_s = kept([P, S], U8, "v_s")
-        w_raw = {(a, b): kept([P, PACK, HALF], F32, f"w_raw{a}{b}") for a in range(2) for b in range(2)}
-        w_bb = [kept([P, 2, PACK * HALF], BF16, f"w_b{b}") for b in range(2)]
-        w_b = {(a, b): w_bb[b][:, a, :] for a in range(2) for b in range(2)}
-        w_qq = [kept([P, 2 * HALF], U32, f"w_q{b}") for b in range(2)]
-        w_q = {(a, b): w_qq[b][:, HALF * a : HALF * (a + 1)] for a in range(2) for b in range(2)}
-        w_ss = [kept([P, 2 * HALF], U8, f"w_s{b}") for b in range(2)]
-        w_s = {(a, b): w_ss[b][:, HALF * a : HALF * (a + 1)] for a in range(2) for b in range(2)}
-        ld = {(b, u): kept([P, PACK, HALF], F32, f"ld{b}{u}") for b in range(2) for u in range(2)}
-        h_q = {(b, u): kept([P, HALF], U32, f"h_q{b}{u}") for b in range(2) for u in range(2)}
-        h_s = {(b, u): kept([P, HALF], U8, f"h_s{b}{u}") for b in range(2) for u in range(2)}
+        w_raw = {(a, b): kept([P, PACK, HALF], F32, f"w_raw{a}{b}") for a, b in ((0, 0), (0, 1), (1, 1))}
+        w_raw[1, 0] = twice.tile([P, PACK, HALF], F32, name="w_raw10", offset=0)
+        w_round = [kept([P, 2, PACK * HALF], BF16, f"w_round{b}") for b in TWO]
+        w_q = [kept([P, 2 * HALF], U32, f"w_q{b}") for b in TWO]
+        w_s = [kept([P, 2 * HALF], U8, f"w_s{b}") for b in TWO]
+        load_sb = {(b, u): kept([P, PACK, HALF], F32, f"load{b}{u}") for b in TWO for u in TWO}
+        h_q = {(b, u): kept([P, HALF], U32, f"h_q{b}{u}") for b in TWO for u in TWO}
+        h_s = {(b, u): kept([P, HALF], U8, f"h_s{b}{u}") for b in TWO for u in TWO}
         b8_raw = kept([P, 2 * N], U32, "b8_raw")
         b8_w = kept([P, 2 * N], U32, "b8_w")
         a4_raw = kept([P, 4 * N], U8, "a4_raw")
         a4_w = kept([P, 4 * N], U8, "a4_w")
-        a4s_raw = kept([P, 2 * N], U8, "a4s_raw")
-        a4_s = kept([P, 2 * N], U8, "a4_s")
-        d_sb = [kept([P, S], F32, f"d_sb{t}") for t in range(PACK)]
-        e_sb = [kept([P, S], F32, f"e_sb{t}") for t in range(PACK)]
-        third = [w_raw[1, 1][:, t, :] for t in range(PACK)]
-        picked = [w_b[0, 0].bitcast(F32)[:, 0:PICK], w_b[1, 0].bitcast(F32)[:, 0:PICK], ld[0, 0][:, 0, :], ld[0, 0][:, 1, :]]
-        pairs = [w_bb[0][:].bitcast(F32)[:, :, 0:PICK], ld[0, 0][:, 0:2, :]]
+        ab_s_raw = kept([P, 2 * N], U8, "ab_s_raw")
+        ab_s = kept([P, 2 * N], U8, "ab_s")
+        d_sb = [kept([P, S], F32, f"d_sb{t}") for t in TWO]
+        d_sb.extend(twice.tile([P, S], F32, name=f"d_sb{2 + i}", offset=4 * S * i) for i in TWO)
+        e_sb = [kept([P, S], F32, f"e_sb{t}") for t in SLICES]
+        picked = [w_round[0][:].bitcast(F32)[:, :, 0:PICK], load_sb[0, 0][:, 0:2, :]]
+        sine = w_raw[1, 1]
+        ripple = load_sb[1, 1]
         square = kept([P, PACK, PICK], F32, "square")
         sat = kept([P, PACK, PICK], F32, "sat")
         y = kept([P, 2, PACK, QUART], F32, "y")
-        y_b = [kept([P, PACK * QUART], BF16, f"y_b{u}") for u in range(2)]
+        y_round = [kept([P, PACK * QUART], BF16, f"y_round{u}") for u in TWO]
         y_q = kept([P, PICK], U32, "y_q")
         y_s = kept([P, PICK], U8, "y_s")
-        rows = {name: kept([P, PACK], F32, name) for name in
-                ("slope_sb", "thr_sb", "tilt_sb", "gain_sb", "gain_tilt", "gain3", "gain4", "root", "halves")}
+        row = {name: kept([P, PACK], F32, name) for name in
+               ("slope", "thr", "tilt", "gain", "gain_tilt", "gain3", "gain4", "root", "halves")}
 
         nc.gpsimd.memset(tab_s[:].bitcast(I32), 0)
-        nc.gpsimd.memset(a4s_raw[:].bitcast(I32), 0)
-        nc.gpsimd.memset(rows["halves"][:], 0.5)
+        nc.gpsimd.memset(ab_s_raw[:].bitcast(I32), 0)
+        nc.gpsimd.memset(row["halves"][:], 0.5)
 
-        def load_words(dst, src):
-            nc.sync.dma_start(out=dst[:].bitcast(I32), in_=src.rearrange("p n t -> p (n t)").bitcast(I32))
+        def load_table(a):
+            nc.sync.dma_start(out=tab_w[a][:].bitcast(I32), in_=tab_words[a].rearrange("p n i -> p (n i)").bitcast(I32))
 
         def load_w(a, b):
-            nc.sync.dma_start(out=w_raw[a, b][:], in_=w1[PASS * a : PASS * (a + 1), HALF * b : HALF * (b + 1)].rearrange("(p j) c -> p j c", j=PACK))
+            block = w1[PASS * a : PASS * (a + 1), HALF * b : HALF * (b + 1)]
+            nc.sync.dma_start(out=w_raw[a, b][:], in_=block.rearrange("(p i) c -> p i c", i=PACK))
 
-        def load_ld(b, u):
-            nc.sync.dma_start(out=ld[b, u][:], in_=load[PASS * b : PASS * (b + 1), HALF * u : HALF * (u + 1)].rearrange("(p t) s -> p t s", t=PACK))
-
-        def load_row(name, vec):
-            nc.gpsimd.dma_start(out=rows[name][:], in_=vec.rearrange("(p t) -> p t", t=PACK))
+        def load_load(b, u):
+            block = load[PASS * b : PASS * (b + 1), HALF * u : HALF * (u + 1)]
+            nc.sync.dma_start(out=load_sb[b, u][:], in_=block.rearrange("(p t) s -> p t s", t=PACK))
 
         nc.sync.dma_start(offs_sb[:], offs)
         nc.sync.dma_start(pos2_sb[:], pos2)
-        for q in range(4):
-            nc.sync.dma_start(out=tab_s[32 * q : 32 * q + 8, :].bitcast(I32), in_=tab_scales[:, 4 * q : 4 * q + 4, :].bitcast(I32))
-        load_words(tab_w[0], tab_words[0])
-        for q in range(4):
-            nc.sync.dma_start(out=a4s_raw[32 * q : 32 * q + 4, :].bitcast(I32).rearrange("r (a c) -> r a c", a=2),
-                              in_=a4_scales[:, 4 * q : 4 * q + 4, :].rearrange("a r c -> r a c").bitcast(I32))
-        load_words(tab_w[1], tab_words[1])
-        for q in range(4):
-            nc.sync.dma_start(out=a4s_raw[32 * q + 4 : 32 * q + 12, 0:N].bitcast(I32), in_=b8_scales[:, 4 * q : 4 * q + 4, :].bitcast(I32))
+        for q in QUADRANTS:
+            nc.sync.dma_start(out=tab_s[32 * q : 32 * q + 8, :].bitcast(I32),
+                              in_=tab_scales[:, 4 * q : 4 * q + 4, :].bitcast(I32))
+        load_table(0)
+        for q in QUADRANTS:
+            nc.sync.dma_start(out=ab_s_raw[32 * q : 32 * q + 4, :].bitcast(I32).rearrange("r (b c) -> r b c", b=2),
+                              in_=a4_scales[:, 4 * q : 4 * q + 4, :].rearrange("b r c -> r b c").bitcast(I32))
+        load_table(1)
+        for q in QUADRANTS:
+            nc.sync.dma_start(out=ab_s_raw[32 * q + 4 : 32 * q + 12, 0:N].bitcast(I32),
+                              in_=b8_scales[:, 4 * q : 4 * q + 4, :].bitcast(I32))
         nc.sync.dma_start(out=b8_raw[:].bitcast(I32).rearrange("p (a n) -> p a n", a=2),
-                          in_=b8_words.rearrange("a p n t -> p a (n t)").bitcast(I32))
+                          in_=b8_words.rearrange("a p n i -> p a (n i)").bitcast(I32))
         load_w(0, 0)
         load_w(1, 0)
-        load_ld(0, 0)
+        load_load(0, 0)
         load_w(0, 1)
         load_w(1, 1)
-        nc.sync.dma_start(out=a4_raw[:].bitcast(I32).rearrange("p (a n) -> p a n", a=2),
-                          in_=a4_words.rearrange("a p n -> p a n").bitcast(I32))
-        load_ld(0, 1)
-        load_ld(1, 0)
+        nc.sync.dma_start(out=a4_raw[:].bitcast(I32).rearrange("p (b n) -> p b n", b=2),
+                          in_=a4_words.rearrange("b p n -> p b n").bitcast(I32))
+        load_load(0, 1)
+        load_load(1, 0)
         nc.sync.dma_start(pos1_sb[:], pos1)
-        load_ld(1, 1)
-        load_row("gain_sb", gain)
-        load_row("tilt_sb", tilt)
-        load_row("slope_sb", slope)
-        load_row("thr_sb", thr)
+        load_load(1, 1)
+        for name, vec in (("gain", gain), ("tilt", tilt), ("slope", slope), ("thr", thr)):
+            nc.gpsimd.dma_start(out=row[name][:], in_=vec.rearrange("(p t) -> p t", t=PACK))
 
-        nc.gpsimd.tensor_scalar(rows["gain4"][:], rows["gain_sb"][:], 4.0, 0.0, ALU.mult, ALU.add)
-        nc.gpsimd.tensor_scalar(rows["gain3"][:], rows["gain_sb"][:], 3.0, 0.0, ALU.mult, ALU.add)
-        nc.gpsimd.tensor_tensor(rows["root"][:], rows["gain4"][:], rows["halves"][:], ALU.pow)
-        nc.gpsimd.tensor_tensor(rows["gain_tilt"][:], rows["gain_sb"][:], rows["tilt_sb"][:], ALU.mult)
+        nc.gpsimd.tensor_scalar(row["gain4"][:], row["gain"][:], 4.0, 0.0, ALU.mult, ALU.add)
+        nc.gpsimd.tensor_scalar(row["gain3"][:], row["gain"][:], 3.0, 0.0, ALU.mult, ALU.add)
+        nc.gpsimd.tensor_tensor(row["root"][:], row["gain4"][:], row["halves"][:], ALU.pow)
+        nc.gpsimd.tensor_tensor(row["gain_tilt"][:], row["gain"][:], row["tilt"][:], ALU.mult)
 
-        def prepare_w(a, b, copies):
-            rounded = w_b[a, b]
-            if copies[0] is None:
-                copies[1](out=rounded.rearrange("p (t m j) -> p m j t", t=PACK, j=PACK), in_=w_raw[a, b][:].rearrange("p j (m t) -> p m j t", t=PACK))
-            for g, copy in enumerate(copies if copies[0] else ()):
-                copy(out=rounded.rearrange("p (t m j) -> p m j t", t=PACK, j=PACK)[:, :, :, 2 * g : 2 * g + 2],
-                     in_=w_raw[a, b][:].rearrange("p j (m t) -> p m j t", t=PACK)[:, :, :, 2 * g : 2 * g + 2])
-            if b not in (1,):
-                nc.vector.quantize_mx(out=w_q[a, b].bitcast(FP8X4), scales=w_s[a, b], in_=rounded)
-            elif a == 1:
-                nc.vector.quantize_mx(out=w_qq[b][:].bitcast(FP8X4), scales=w_ss[b][:], in_=w_bb[b][:].rearrange("p a c -> p (a c)"))
+        def deal(copy, dst, src, run):
+            copy(out=dst.rearrange("p (a t m e) -> p a m t e", a=2, t=PACK, e=run),
+                 in_=src.rearrange("p (a m e t) -> p a m t e", a=2, t=PACK, e=run))
+
+        def quantise_w(a, b, copies):
+            dst = w_round[b][:, a, :].rearrange("p (t m i) -> p m i t", t=PACK, i=PACK)
+            src = w_raw[a, b][:].rearrange("p i (m t) -> p m i t", t=PACK)
+            share = PACK // len(copies)
+            for n, copy in enumerate(copies):
+                copy(out=dst[:, :, :, share * n : share * (n + 1)], in_=src[:, :, :, share * n : share * (n + 1)])
+            cols = slice(HALF * a, HALF * (a + 1))
+            nc.vector.quantize_mx(out=w_q[b][:, cols].bitcast(FP8X4), scales=w_s[b][:, cols], in_=w_round[b][:, a, :])
 
         def v_operands(a, cols):
             return dict(rhs=v_w[a][:, cols].bitcast(FP8X4), rhs_scale=v_s[4 * a : P, cols])
 
-        wide = {}
+        def make_d(t):
+            for u in TWO:
+                cols = slice(HALF * u, HALF * (u + 1))
+                bank = mixed_banks.tile([P, HALF], F32, name="bank")
+                for a in TWO:
+                    nc.tensor.matmul_mx(out=bank[:], lhsT=b8_w[:, N * a + P * t : N * a + P * (t + 1)].bitcast(FP8X4),
+                                        lhsT_scale=ab_s[4 + 4 * a : P, P * t : P * (t + 1)],
+                                        start=(a == 0), stop=(a == 1), **v_operands(a, cols))
+                nc.scalar.copy(out=d_sb[t][:, cols], in_=bank[:])
+
+        h_round = {}
 
         def make_h(b, u, k):
             if k == 0:
-                wide[b, u] = ring.tile([P, PACK * HALF], BF16, name="h_b", align_bytes=64)
-            rounded = wide[b, u][:, PACK * QUART * k : PACK * QUART * (k + 1)]
-            for i in range(2):
-                c0 = QUART * k + P * i
-                bank = acc.tile([P, PACK, P], F32, name="bank") if (b, u) == (0, 1) else hps.tile([P, PACK, P], F32, name="h_bank")
-                steps = [(a, t) for a in range(2) for t in range(PACK)] if (b, u) == (1, 0) else [(a, t) for t in range(PACK) for a in range(2)]
+                h_round[b, u] = ring.tile([P, PACK * HALF], BF16, name="h_round", align_bytes=64)
+            by_pass = (b, u) == (1, 0)
+            steps = [(a, t) for a in TWO for t in SLICES] if by_pass else [(a, t) for t in SLICES for a in TWO]
+            for c0 in range(QUART * k, QUART * (k + 1), P):
+                if (b, u) == (0, 1):
+                    bank = mixed_banks.tile([P, PACK, P], F32, name="bank")
+                else:
+                    bank = h_banks.tile([P, PACK, P], F32, name="h_bank")
                 for n, (a, t) in enumerate(steps):
-                    if True:
-                        nc.tensor.matmul_mx(out=bank[:, t, :], lhsT=w_q[a, b][:, P * t : P * (t + 1)].bitcast(FP8X4),
-                                            lhsT_scale=w_s[a, b][:, P * t : P * (t + 1)],
-                                            start=(n == 0), stop=(n == len(steps) - 1),
-                                            **v_operands(a, slice(HALF * u + c0, HALF * u + c0 + P)))
+                    w_cols = slice(HALF * a + P * t, HALF * a + P * (t + 1))
+                    nc.tensor.matmul_mx(out=bank[:, t, :], lhsT=w_q[b][:, w_cols].bitcast(FP8X4), lhsT_scale=w_s[b][:, w_cols],
+                                        start=(n == 0), stop=(n == len(steps) - 1),
+                                        **v_operands(a, slice(HALF * u + c0, HALF * u + c0 + P)))
                 nc.vector.tensor_tensor(
-                    out=rounded[:, PASS * i : PASS * (i + 1)].rearrange("p (c e t) -> p c t e", e=2, t=PACK),
+                    out=h_round[b, u][:, PACK * c0 : PACK * (c0 + P)].rearrange("p (c e t) -> p c t e", e=2, t=PACK),
                     in0=bank[:].rearrange("p t (c e) -> p c t e", e=2),
-                    in1=ld[b, u][:, :, c0 : c0 + P].rearrange("p t (c e) -> p c t e", e=2),
+                    in1=load_sb[b, u][:, :, c0 : c0 + P].rearrange("p t (c e) -> p c t e", e=2),
                     op=ALU.mult)
+
+        def quantise_h(b, u, c0, c1):
+            nc.vector.quantize_mx(out=h_q[b, u][:, c0:c1].bitcast(FP8X4), scales=h_s[b, u][:, c0:c1],
+                                  in_=h_round[b, u][:, PACK * c0 : PACK * c1])
+
+        e_banks = {}
+
+        def e_pass(n, b):
+            u, k = divmod(n, 2)
             cols = slice(QUART * k, QUART * (k + 1))
-            if b == 1:
-                nc.vector.quantize_mx(out=h_q[b, u][:, cols].bitcast(FP8X4), scales=h_s[b, u][:, cols], in_=rounded)
-            elif k == 1:
-                nc.vector.quantize_mx(out=h_q[b, u][:].bitcast(FP8X4), scales=h_s[b, u][:], in_=wide[b, u][:])
+            for g in TWO:
+                if b == 0:
+                    e_banks[n, g] = mixed_banks.tile([P, 2, QUART], F32, name="bank")
+                for i in TWO:
+                    c0 = N * b + P * (2 * g + i)
+                    nc.tensor.matmul_mx(out=e_banks[n, g][:, i, :], lhsT=a4_w[:, 2 * c0 : 2 * (c0 + P)].bitcast(FP4X4),
+                                        lhsT_scale=ab_s[:, c0 : c0 + P], rhs=h_q[b, u][:, cols].bitcast(FP8X4),
+                                        rhs_scale=h_s[b, u][:, cols], start=(b == 0 and i == 0), stop=(b == 1 and i == 1))
 
-        def e_pass(out, t, b, u, cols, start, stop):
-            c0 = N * b + P * t
-            nc.tensor.matmul_mx(out=out, lhsT=a4_w[:, 2 * c0 : 2 * (c0 + P)].bitcast(FP4X4), lhsT_scale=a4_s[:, c0 : c0 + P],
-                                rhs=h_q[b, u][:, cols].bitcast(FP8X4), rhs_scale=h_s[b, u][:, cols], start=start, stop=stop)
+        def fetch_e(n, copies):
+            for t, copy in enumerate(copies):
+                copy(out=e_sb[t][:, QUART * n : QUART * (n + 1)], in_=e_banks[n, t // 2][:, t % 2, :])
 
-        def make_d(t):
-            for u in range(2):
-                bank = acc.tile([P, HALF], F32, name="bank")
-                for a in range(2):
-                    nc.tensor.matmul_mx(out=bank[:], lhsT=b8_w[:, N * a + P * t : N * a + P * (t + 1)].bitcast(FP8X4),
-                                        lhsT_scale=a4_s[4 + 4 * a : P, P * t : P * (t + 1)],
-                                        start=(a == 0), stop=(a == 1), **v_operands(a, slice(HALF * u, HALF * (u + 1))))
-                nc.scalar.copy(out=d_sb[t][:, HALF * u : HALF * (u + 1)], in_=bank[:])
-
-        def sine(t):
-            if t % 2 == 0:
-                nc.scalar.activation(out=w_raw[1, 1][:, t : t + 2, :], in_=pairs[t // 2], func=ACT.Sin, scale=-1.0 / 3.0)
-            nc.scalar.activation(out=square[:, t, :], in_=third[t], func=ACT.Square, scale=rows["root"][:, t : t + 1])
-
-        banks = {}
-
-        def open_e(n):
-            u, k = divmod(n, 2)
-            for g in range(2):
-                banks[n, g] = acc.tile([P, 2, QUART], F32, name="bank")
-                for i in range(2):
-                    e_pass(banks[n, g][:, i, :], 2 * g + i, 0, u, slice(QUART * k, QUART * (k + 1)), i == 0, False)
-
-        def close_e(n, copy):
-            u, k = divmod(n, 2)
-            for g in range(2):
-                for i in range(2):
-                    e_pass(banks[n, g][:, i, :], 2 * g + i, 1, u, slice(QUART * k, QUART * (k + 1)), False, i == 1)
-            for t in range(PACK):
-                (copy if n < 3 else (nc.scalar.copy, nc.vector.tensor_copy, nc.vector.tensor_copy, nc.vector.tensor_copy)[t])(out=e_sb[t][:, QUART * n : QUART * (n + 1)], in_=banks[n, t // 2][:, t % 2, :])
+        on_scalar, on_vector = nc.scalar.copy, nc.vector.tensor_copy
 
         nc.vector.tensor_copy(out=v_s[:], in_=tab_s[:].indirect(offs_sb[:]))
-        nc.vector.tensor_copy(out=v_w[0][:], in_=tab_w[0][:].indirect(offs_sb[:]))
-        nc.vector.tensor_copy(out=v_w[1][:], in_=tab_w[1][:].indirect(offs_sb[:]))
-        nc.scalar.copy(out=b8_w[:].rearrange("p (a t m e) -> p a m t e", a=2, t=PACK, e=4),
-                       in_=b8_raw[:].rearrange("p (a m e t) -> p a m t e", a=2, t=PACK, e=4))
-        nc.vector.tensor_copy(out=a4_s[:].rearrange("p (a t m e) -> p a m t e", a=2, t=PACK, e=16),
-                              in_=a4s_raw[:].rearrange("p (a m e t) -> p a m t e", a=2, t=PACK, e=16))
-        prepare_w(0, 0, (None, nc.vector.tensor_copy))
-        prepare_w(1, 0, (nc.scalar.copy, nc.vector.tensor_copy))
-        make_d(0)
-        make_d(1)
-        make_d(2)
-        make_d(3)
-        make_h(0, 0, 0)
-        make_h(0, 0, 1)
-        prepare_w(0, 1, (None, nc.scalar.copy))
-        prepare_w(1, 1, (None, nc.scalar.copy))
-        nc.scalar.copy(out=a4_w[:].bitcast(U16).rearrange("p (a t m e) -> p a m t e", a=2, t=PACK, e=8),
-                       in_=a4_raw[:].bitcast(U16).rearrange("p (a m e t) -> p a m t e", a=2, t=PACK, e=8))
-        make_h(0, 1, 0)
-        make_h(0, 1, 1)
-        nc.vector.tensor_copy(out=picked[0], in_=d_sb[0][:].indirect(pos2_sb[:]))
-        nc.vector.tensor_copy(out=picked[1], in_=d_sb[1][:].indirect(pos2_sb[:]))
-        nc.vector.tensor_copy(out=picked[2], in_=d_sb[2][:].indirect(pos2_sb[:]))
-        nc.vector.tensor_copy(out=picked[3], in_=d_sb[3][:].indirect(pos2_sb[:]))
-        make_h(1, 0, 0)
-        open_e(0)
-        open_e(1)
-        sine(0)
-        sine(1)
-        sine(2)
-        sine(3)
-        close_e(0, nc.scalar.copy)
-        make_h(1, 0, 1)
-        close_e(1, nc.scalar.copy)
-        make_h(1, 1, 0)
-        open_e(2)
-        close_e(2, nc.scalar.copy)
-        make_h(1, 1, 1)
-        open_e(3)
-        close_e(3, nc.vector.tensor_copy)
+        for a in TWO:
+            nc.vector.tensor_copy(out=v_w[a][:], in_=tab_w[a][:].indirect(offs_sb[:]))
+        deal(on_scalar, b8_w[:], b8_raw[:], 4)
+        deal(on_vector, ab_s[:], ab_s_raw[:], 16)
+        quantise_w(0, 0, [on_vector])
+        quantise_w(1, 0, [on_scalar, on_vector])
+        for t in SLICES:
+            make_d(t)
+        for k in TWO:
+            make_h(0, 0, k)
+        quantise_h(0, 0, 0, HALF)
+        for t in SLICES:
+            nc.vector.tensor_copy(out=picked[t // 2][:, t % 2, :], in_=d_sb[t][:].indirect(pos2_sb[:]))
+        quantise_w(0, 1, [on_scalar])
+        quantise_w(1, 1, [on_scalar])
+        deal(on_scalar, a4_w[:].bitcast(U16), a4_raw[:].bitcast(U16), 8)
+        for k in TWO:
+            make_h(0, 1, k)
+        quantise_h(0, 1, 0, HALF)
 
-        ripple = ld[1, 1]
-        for t in range(PACK):
-            nc.vector.scalar_tensor_tensor(out=ripple[:, t, :], in0=square[:, t, :], scalar=rows["gain3"][:, t : t + 1],
-                                           in1=third[t], op0=ALU.subtract, op1=ALU.mult)
+        make_h(1, 0, 0)
+        quantise_h(1, 0, 0, QUART)
+        e_pass(0, 0)
+        e_pass(1, 0)
+        for t in SLICES:
+            if t % 2 == 0:
+                nc.scalar.activation(out=sine[:, t : t + 2, :], in_=picked[t // 2], func=ACT.Sin, scale=-1.0 / 3.0)
+            nc.scalar.activation(out=square[:, t, :], in_=sine[:, t, :], func=ACT.Square, scale=row["root"][:, t : t + 1])
+        e_pass(0, 1)
+        fetch_e(0, [on_scalar] * PACK)
+        make_h(1, 0, 1)
+        quantise_h(1, 0, QUART, HALF)
+        e_pass(1, 1)
+        fetch_e(1, [on_scalar] * PACK)
+        for k in TWO:
+            make_h(1, 1, k)
+            quantise_h(1, 1, QUART * k, QUART * (k + 1))
+            e_pass(2 + k, 0)
+            e_pass(2 + k, 1)
+            fetch_e(2 + k, [on_scalar] * PACK if k == 0 else [on_scalar] + [on_vector] * (PACK - 1))
+
+        for t in SLICES:
+            nc.vector.scalar_tensor_tensor(out=ripple[:, t, :], in0=square[:, t, :], scalar=row["gain3"][:, t : t + 1],
+                                           in1=sine[:, t, :], op0=ALU.subtract, op1=ALU.mult)
+
         out_rows = out_0.rearrange("(p t) m -> p t m", t=PACK)
         out_words = out_1[0].rearrange("p m t -> p (m t)").bitcast(I32)
 
         def look(t, u0, u1):
             c0, c1 = QUART * u0, QUART * u1
-            nc.scalar.activation(out=sat[:, t, c0:c1], in_=e_sb[t][:].indirect(pos1_sb[:, c0 // 16 : c1 // 16]), func=ACT.Sigmoid,
-                                 bias=rows["thr_sb"][:, t : t + 1], scale=rows["slope_sb"][:, t : t + 1])
-            nc.vector.scalar_tensor_tensor(out=y[:, u0:u1, t, :], in0=sat[:, t, c0:c1].rearrange("p (u c) -> p u c", c=QUART), scalar=rows["gain_tilt"][:, t : t + 1],
-                                           in1=ripple[:, t, c0:c1].rearrange("p (u c) -> p u c", c=QUART), op0=ALU.mult, op1=ALU.min)
+            nc.scalar.activation(out=sat[:, t, c0:c1], in_=e_sb[t][:].indirect(pos1_sb[:, c0 // 16 : c1 // 16]),
+                                 func=ACT.Sigmoid, bias=row["thr"][:, t : t + 1], scale=row["slope"][:, t : t + 1])
+            nc.vector.scalar_tensor_tensor(out=y[:, u0:u1, t, :], in0=sat[:, t, c0:c1].rearrange("p (u c) -> p u c", c=QUART),
+                                           scalar=row["gain_tilt"][:, t : t + 1],
+                                           in1=ripple[:, t, c0:c1].rearrange("p (u c) -> p u c", c=QUART),
+                                           op0=ALU.mult, op1=ALU.min)
 
-        def store(u, t0, t1):
+        def store_y(u, t0, t1):
             nc.sync.dma_start(out=out_rows[:, t0:t1, QUART * u : QUART * (u + 1)], in_=y[:, u, t0:t1, :])
 
-        def planes(u):
-            cols = slice(QUART * u, QUART * (u + 1))
-            (nc.scalar.copy, nc.vector.tensor_copy)[u](out=y_b[u][:].rearrange("p (c e t) -> p c t e", e=2, t=PACK),
-                                  in_=y[:, u, :, :].rearrange("p t (c e) -> p c t e", e=2))
-            nc.vector.quantize_mx(out=y_q[:, cols].bitcast(FP8X4), scales=y_s[:, cols], in_=y_b[u][:])
-            (nc.sync, nc.scalar)[u].dma_start(out=out_words[:, cols], in_=y_q[:, cols].bitcast(I32))
-
-        WIDE = 2
-        for t in range(WIDE):
+        for t in TWO:
             look(t, 0, 2)
-        for u in range(2):
-            for t in range(WIDE, PACK):
-                look(t, u, u + 1)
-                if t == 1:
-                    store(u, 0, 2)
-            if WIDE >= 2 and u == 0:
-                store(1, 0, WIDE)
-            store(u, (0 if u == 0 else WIDE) if WIDE >= 2 else 2, PACK)
-        planes(0)
-        planes(1)
-        for q in range(4):
-            eng = nc.sync if q < 3 else nc.scalar
-            eng.dma_start(out=out_2[0, 4 * q : 4 * q + 4, :].bitcast(I32), in_=y_s[32 * q : 32 * q + 4, :].bitcast(I32))
+        for t in (2, 3):
+            look(t, 0, 1)
+        store_y(1, 0, 2)
+        store_y(0, 0, PACK)
+        for t in (2, 3):
+            look(t, 1, 2)
+        store_y(1, 2, PACK)
+
+        for u, copy, queue in ((0, on_scalar, nc.sync), (1, on_vector, nc.scalar)):
+            cols = slice(QUART * u, QUART * (u + 1))
+            copy(out=y_round[u][:].rearrange("p (c e t) -> p c t e", e=2, t=PACK),
+                 in_=y[:, u, :, :].rearrange("p t (c e) -> p c t e", e=2))
+            nc.vector.quantize_mx(out=y_q[:, cols].bitcast(FP8X4), scales=y_s[:, cols], in_=y_round[u][:])
+            queue.dma_start(out=out_words[:, cols], in_=y_q[:, cols].bitcast(I32))
+        for q, queue in zip(QUADRANTS, (nc.sync, nc.sync, nc.sync, nc.scalar)):
+            queue.dma_start(out=out_2[0, 4 * q : 4 * q + 4, :].bitcast(I32), in_=y_s[32 * q : 32 * q + 4, :].bitcast(I32))

from contextlib import ExitStack

import concourse.mybir as mybir

K, H, N, T, S, PICK = 1024, 1024, 512, 2048, 1024, 512
FLOPS = 2 * K * H * S + 2 * H * N * S + 2 * K * N * S

F32 = mybir.dt.float32
BF16 = mybir.dt.bfloat16
I32 = mybir.dt.int32
U32 = mybir.dt.uint32
U16 = mybir.dt.uint16
U8 = mybir.dt.uint8
FP8X4 = mybir.dt.float8_e4m3fn_x4
FP4X4 = mybir.dt.float4_e2m1fn_x4
ALU = mybir.AluOpType
ACT = mybir.ActivationFunctionType

P = 128
PACK = 4
PASS = P * PACK
HALF = 512
QUART = 256
TWO = range(2)
QUADRANTS = range(4)
SLICES = range(PACK)


def tile_list_amplifier_channel_scores_kernel(
    tc, tab_words, tab_scales, offs, pos1, pos2, w1, load, a4_words, a4_scales,
    b8_words, b8_scales, slope, thr, tilt, gain, out_0, out_1, out_2,
):
    nc = tc.nc
    with ExitStack() as ctx:
        keep = ctx.enter_context(tc.tile_pool(name="keep", bufs=1))
        twice = ctx.enter_context(tc.tile_pool(name="twice", bufs=1))
        ring = ctx.enter_context(tc.tile_pool(name="ring", bufs=2))
        mixed_banks = ctx.enter_context(tc.psum_pool(name="mixed_banks", bufs=4))
        h_banks = ctx.enter_context(tc.psum_pool(name="h_banks", bufs=4))

        def kept(shape, dtype, name):
            return keep.tile(shape, dtype, name=name, align_bytes=64)

        offs_sb = keep.tile([P, S // 16], U16, name="offs_sb")
        pos1_sb = keep.tile([P, PICK // 16], U16, name="pos1_sb")
        pos2_sb = keep.tile([P, PICK // 16], U16, name="pos2_sb")
        tab_w = [kept([P, T], U32, f"tab_w{a}") for a in TWO]
        tab_s = kept([P, T], U8, "tab_s")
        v_w = [kept([P, S], U32, f"v_w{a}") for a in TWO]
        v_s = kept([P, S], U8, "v_s")
        w_raw = {(a, b): kept([P, PACK, HALF], F32, f"w_raw{a}{b}") for a, b in ((0, 0), (0, 1), (1, 1))}
        w_raw[1, 0] = twice.tile([P, PACK, HALF], F32, name="w_raw10", offset=0)
        w_round = [kept([P, 2, PACK * HALF], BF16, f"w_round{b}") for b in TWO]
        w_q = [kept([P, 2 * HALF], U32, f"w_q{b}") for b in TWO]
        w_s = [kept([P, 2 * HALF], U8, f"w_s{b}") for b in TWO]
        load_sb = {(b, u): kept([P, PACK, HALF], F32, f"load{b}{u}") for b in TWO for u in TWO}
        h_q = {(b, u): kept([P, HALF], U32, f"h_q{b}{u}") for b in TWO for u in TWO}
        h_s = {(b, u): kept([P, HALF], U8, f"h_s{b}{u}") for b in TWO for u in TWO}
        b8_raw = kept([P, 2 * N], U32, "b8_raw")
        b8_w = kept([P, 2 * N], U32, "b8_w")
        a4_raw = kept([P, 4 * N], U8, "a4_raw")
        a4_w = kept([P, 4 * N], U8, "a4_w")
        ab_s_raw = kept([P, 2 * N], U8, "ab_s_raw")
        ab_s = kept([P, 2 * N], U8, "ab_s")
        d_sb = [kept([P, S], F32, f"d_sb{t}") for t in TWO]
        d_sb.extend(twice.tile([P, S], F32, name=f"d_sb{2 + i}", offset=4 * S * i) for i in TWO)
        e_sb = [kept([P, S], F32, f"e_sb{t}") for t in SLICES]
        picked = [w_round[0][:].bitcast(F32)[:, :, 0:PICK], load_sb[0, 0][:, 0:2, :]]
        sine = w_raw[1, 1]
        ripple = load_sb[1, 1]
        square = kept([P, PACK, PICK], F32, "square")
        sat = kept([P, PACK, PICK], F32, "sat")
        y = kept([P, 2, PACK, QUART], F32, "y")
        y_round = [kept([P, PACK * QUART], BF16, f"y_round{u}") for u in TWO]
        y_q = kept([P, PICK], U32, "y_q")
        y_s = kept([P, PICK], U8, "y_s")
        row = {name: kept([P, PACK], F32, name) for name in
               ("slope", "thr", "tilt", "gain", "gain_tilt", "gain3", "gain4", "root", "halves")}

        nc.gpsimd.memset(tab_s[:].bitcast(I32), 0)
        nc.gpsimd.memset(ab_s_raw[:].bitcast(I32), 0)
        nc.gpsimd.memset(row["halves"][:], 0.5)

        def load_table(a):
            nc.sync.dma_start(out=tab_w[a][:].bitcast(I32), in_=tab_words[a].rearrange("p n i -> p (n i)").bitcast(I32))

        def load_w(a, b):
            block = w1[PASS * a : PASS * (a + 1), HALF * b : HALF * (b + 1)]
            nc.sync.dma_start(out=w_raw[a, b][:], in_=block.rearrange("(p i) c -> p i c", i=PACK))

        def load_load(b, u):
            block = load[PASS * b : PASS * (b + 1), HALF * u : HALF * (u + 1)]
            nc.sync.dma_start(out=load_sb[b, u][:], in_=block.rearrange("(p t) s -> p t s", t=PACK))

        nc.sync.dma_start(offs_sb[:], offs)
        nc.sync.dma_start(pos2_sb[:], pos2)
        for q in QUADRANTS:
            nc.sync.dma_start(out=tab_s[32 * q : 32 * q + 8, :].bitcast(I32),
                              in_=tab_scales[:, 4 * q : 4 * q + 4, :].bitcast(I32))
        load_table(0)
        for q in QUADRANTS:
            nc.sync.dma_start(out=ab_s_raw[32 * q : 32 * q + 4, :].bitcast(I32).rearrange("r (b c) -> r b c", b=2),
                              in_=a4_scales[:, 4 * q : 4 * q + 4, :].rearrange("b r c -> r b c").bitcast(I32))
        load_table(1)
        for q in QUADRANTS:
            nc.sync.dma_start(out=ab_s_raw[32 * q + 4 : 32 * q + 12, 0:N].bitcast(I32),
                              in_=b8_scales[:, 4 * q : 4 * q + 4, :].bitcast(I32))
        nc.sync.dma_start(out=b8_raw[:].bitcast(I32).rearrange("p (a n) -> p a n", a=2),
                          in_=b8_words.rearrange("a p n i -> p a (n i)").bitcast(I32))
        load_w(0, 0)
        load_w(1, 0)
        load_load(0, 0)
        load_w(0, 1)
        load_w(1, 1)
        nc.sync.dma_start(out=a4_raw[:].bitcast(I32).rearrange("p (b n) -> p b n", b=2),
                          in_=a4_words.rearrange("b p n -> p b n").bitcast(I32))
        load_load(0, 1)
        load_load(1, 0)
        nc.sync.dma_start(pos1_sb[:], pos1)
        load_load(1, 1)
        for name, vec in (("gain", gain), ("tilt", tilt), ("slope", slope), ("thr", thr)):
            nc.gpsimd.dma_start(out=row[name][:], in_=vec.rearrange("(p t) -> p t", t=PACK))

        nc.gpsimd.tensor_scalar(row["gain4"][:], row["gain"][:], 4.0, 0.0, ALU.mult, ALU.add)
        nc.gpsimd.tensor_scalar(row["gain3"][:], row["gain"][:], 3.0, 0.0, ALU.mult, ALU.add)
        nc.gpsimd.tensor_tensor(row["root"][:], row["gain4"][:], row["halves"][:], ALU.pow)
        nc.gpsimd.tensor_tensor(row["gain_tilt"][:], row["gain"][:], row["tilt"][:], ALU.mult)

        def deal(copy, dst, src, run):
            copy(out=dst.rearrange("p (a t m e) -> p a m t e", a=2, t=PACK, e=run),
                 in_=src.rearrange("p (a m e t) -> p a m t e", a=2, t=PACK, e=run))

        def quantise_w(a, b, copies):
            dst = w_round[b][:, a, :].rearrange("p (t m i) -> p m i t", t=PACK, i=PACK)
            src = w_raw[a, b][:].rearrange("p i (m t) -> p m i t", t=PACK)
            share = PACK // len(copies)
            for n, copy in enumerate(copies):
                copy(out=dst[:, :, :, share * n : share * (n + 1)], in_=src[:, :, :, share * n : share * (n + 1)])
            cols = slice(HALF * a, HALF * (a + 1))
            nc.vector.quantize_mx(out=w_q[b][:, cols].bitcast(FP8X4), scales=w_s[b][:, cols], in_=w_round[b][:, a, :])

        def v_operands(a, cols):
            return dict(rhs=v_w[a][:, cols].bitcast(FP8X4), rhs_scale=v_s[4 * a : P, cols])

        def make_d(t):
            for u in TWO:
                cols = slice(HALF * u, HALF * (u + 1))
                bank = mixed_banks.tile([P, HALF], F32, name="bank")
                for a in TWO:
                    nc.tensor.matmul_mx(out=bank[:], lhsT=b8_w[:, N * a + P * t : N * a + P * (t + 1)].bitcast(FP8X4),
                                        lhsT_scale=ab_s[4 + 4 * a : P, P * t : P * (t + 1)],
                                        start=(a == 0), stop=(a == 1), **v_operands(a, cols))
                nc.scalar.copy(out=d_sb[t][:, cols], in_=bank[:])

        h_round = {}

        def make_h(b, u, k):
            if k == 0:
                h_round[b, u] = ring.tile([P, PACK * HALF], BF16, name="h_round", align_bytes=64)
            by_pass = (b, u) == (1, 0)
            steps = [(a, t) for a in TWO for t in SLICES] if by_pass else [(a, t) for t in SLICES for a in TWO]
            for c0 in range(QUART * k, QUART * (k + 1), P):
                if (b, u) == (0, 1):
                    bank = mixed_banks.tile([P, PACK, P], F32, name="bank")
                else:
                    bank = h_banks.tile([P, PACK, P], F32, name="h_bank")
                for n, (a, t) in enumerate(steps):
                    w_cols = slice(HALF * a + P * t, HALF * a + P * (t + 1))
                    nc.tensor.matmul_mx(out=bank[:, t, :], lhsT=w_q[b][:, w_cols].bitcast(FP8X4), lhsT_scale=w_s[b][:, w_cols],
                                        start=(n == 0), stop=(n == len(steps) - 1),
                                        **v_operands(a, slice(HALF * u + c0, HALF * u + c0 + P)))
                nc.vector.tensor_tensor(
                    out=h_round[b, u][:, PACK * c0 : PACK * (c0 + P)].rearrange("p (c e t) -> p c t e", e=2, t=PACK),
                    in0=bank[:].rearrange("p t (c e) -> p c t e", e=2),
                    in1=load_sb[b, u][:, :, c0 : c0 + P].rearrange("p t (c e) -> p c t e", e=2),
                    op=ALU.mult)

        def quantise_h(b, u, c0, c1):
            nc.vector.quantize_mx(out=h_q[b, u][:, c0:c1].bitcast(FP8X4), scales=h_s[b, u][:, c0:c1],
                                  in_=h_round[b, u][:, PACK * c0 : PACK * c1])

        e_banks = {}

        def e_pass(n, b):
            u, k = divmod(n, 2)
            cols = slice(QUART * k, QUART * (k + 1))
            for g in TWO:
                if b == 0:
                    e_banks[n, g] = mixed_banks.tile([P, 2, QUART], F32, name="bank")
                for i in TWO:
                    c0 = N * b + P * (2 * g + i)
                    nc.tensor.matmul_mx(out=e_banks[n, g][:, i, :], lhsT=a4_w[:, 2 * c0 : 2 * (c0 + P)].bitcast(FP4X4),
                                        lhsT_scale=ab_s[:, c0 : c0 + P], rhs=h_q[b, u][:, cols].bitcast(FP8X4),
                                        rhs_scale=h_s[b, u][:, cols], start=(b == 0 and i == 0), stop=(b == 1 and i == 1))

        def fetch_e(n, copies):
            for t, copy in enumerate(copies):
                copy(out=e_sb[t][:, QUART * n : QUART * (n + 1)], in_=e_banks[n, t // 2][:, t % 2, :])

        on_scalar, on_vector = nc.scalar.copy, nc.vector.tensor_copy

        nc.vector.tensor_copy(out=v_s[:], in_=tab_s[:].indirect(offs_sb[:]))
        for a in TWO:
            nc.vector.tensor_copy(out=v_w[a][:], in_=tab_w[a][:].indirect(offs_sb[:]))
        deal(on_scalar, b8_w[:], b8_raw[:], 4)
        deal(on_vector, ab_s[:], ab_s_raw[:], 16)
        quantise_w(0, 0, [on_vector])
        quantise_w(1, 0, [on_scalar, on_vector])
        for t in SLICES:
            make_d(t)
        for k in TWO:
            make_h(0, 0, k)
        quantise_h(0, 0, 0, HALF)
        for t in SLICES:
            nc.vector.tensor_copy(out=picked[t // 2][:, t % 2, :], in_=d_sb[t][:].indirect(pos2_sb[:]))
        quantise_w(0, 1, [on_scalar])
        quantise_w(1, 1, [on_scalar])
        deal(on_scalar, a4_w[:].bitcast(U16), a4_raw[:].bitcast(U16), 8)
        for k in TWO:
            make_h(0, 1, k)
        quantise_h(0, 1, 0, HALF)

        make_h(1, 0, 0)
        quantise_h(1, 0, 0, QUART)
        e_pass(0, 0)
        e_pass(1, 0)
        for t in SLICES:
            if t % 2 == 0:
                nc.scalar.activation(out=sine[:, t : t + 2, :], in_=picked[t // 2], func=ACT.Sin, scale=-1.0 / 3.0)
            nc.scalar.activation(out=square[:, t, :], in_=sine[:, t, :], func=ACT.Square, scale=row["root"][:, t : t + 1])
        e_pass(0, 1)
        fetch_e(0, [on_scalar] * PACK)
        make_h(1, 0, 1)
        quantise_h(1, 0, QUART, HALF)
        e_pass(1, 1)
        fetch_e(1, [on_scalar] * PACK)
        for k in TWO:
            make_h(1, 1, k)
            quantise_h(1, 1, QUART * k, QUART * (k + 1))
            e_pass(2 + k, 0)
            e_pass(2 + k, 1)
            fetch_e(2 + k, [on_scalar] * PACK if k == 0 else [on_scalar] + [on_vector] * (PACK - 1))

        for t in SLICES:
            nc.vector.scalar_tensor_tensor(out=ripple[:, t, :], in0=square[:, t, :], scalar=row["gain3"][:, t : t + 1],
                                           in1=sine[:, t, :], op0=ALU.subtract, op1=ALU.mult)

        out_rows = out_0.rearrange("(p t) m -> p t m", t=PACK)
        out_words = out_1[0].rearrange("p m t -> p (m t)").bitcast(I32)

        def look(t, u0, u1):
            c0, c1 = QUART * u0, QUART * u1
            nc.scalar.activation(out=sat[:, t, c0:c1], in_=e_sb[t][:].indirect(pos1_sb[:, c0 // 16 : c1 // 16]),
                                 func=ACT.Sigmoid, bias=row["thr"][:, t : t + 1], scale=row["slope"][:, t : t + 1])
            nc.vector.scalar_tensor_tensor(out=y[:, u0:u1, t, :], in0=sat[:, t, c0:c1].rearrange("p (u c) -> p u c", c=QUART),
                                           scalar=row["gain_tilt"][:, t : t + 1],
                                           in1=ripple[:, t, c0:c1].rearrange("p (u c) -> p u c", c=QUART),
                                           op0=ALU.mult, op1=ALU.min)

        def store_y(u, t0, t1):
            nc.sync.dma_start(out=out_rows[:, t0:t1, QUART * u : QUART * (u + 1)], in_=y[:, u, t0:t1, :])

        for t in TWO:
            look(t, 0, 2)
        for t in (2, 3):
            look(t, 0, 1)
        store_y(1, 0, 2)
        store_y(0, 0, PACK)
        for t in (2, 3):
            look(t, 1, 2)
        store_y(1, 2, PACK)

        for u, copy, queue in ((0, on_scalar, nc.sync), (1, on_vector, nc.scalar)):
            cols = slice(QUART * u, QUART * (u + 1))
            copy(out=y_round[u][:].rearrange("p (c e t) -> p c t e", e=2, t=PACK),
                 in_=y[:, u, :, :].rearrange("p t (c e) -> p c t e", e=2))
            nc.vector.quantize_mx(out=y_q[:, cols].bitcast(FP8X4), scales=y_s[:, cols], in_=y_round[u][:])
            queue.dma_start(out=out_words[:, cols], in_=y_q[:, cols].bitcast(I32))
        for q, queue in zip(QUADRANTS, (nc.sync, nc.sync, nc.sync, nc.scalar)):
            queue.dma_start(out=out_2[0, 4 * q : 4 * q + 4, :].bitcast(I32), in_=y_s[32 * q : 32 * q + 4, :].bitcast(I32))
